import numpy as np
import ml_dtypes


def mxq(x, axis, fmt="e4m3"):
    dtype, down = {"e4m3": (ml_dtypes.float8_e4m3fn, 7), "e5m2": (ml_dtypes.float8_e5m2, 14)}[fmt]
    v = np.moveaxis(np.asarray(x, np.float32).astype(ml_dtypes.bfloat16).astype(np.float64), axis, -1)
    blocks = v.reshape(v.shape[:-1] + (-1, 32))
    amax = np.abs(blocks).max(-1, keepdims=True)
    byte = np.maximum(np.where(amax > 0, np.frexp(amax)[1] - 1 + 127, 0) - down, 1)
    scale = np.exp2(byte - 127.0)
    codes = (blocks / scale).astype(np.float32).astype(dtype).astype(np.float64)
    return np.moveaxis((codes * scale).reshape(v.shape), -1, axis)


WIDE = False


def mx_kscale(k):
    if not WIDE:
        return np.ones(k)
    levels = np.array([10, -10, 5, -5, 0])
    if k % 512:
        return np.exp2(np.random.permutation(np.resize(levels, k // 32))).repeat(32)
    a = np.empty((k // 512, 16))
    for p in range(k // 512):
        a[p, :8] = np.random.permutation(np.resize(levels, 8))
        for g in range(8):
            far = levels[np.abs(levels - a[p, g]) >= 10]
            a[p, g + 8] = far[np.random.randint(len(far))]
    return np.exp2(a.ravel()).repeat(32)


def f64(x):
    return np.asarray(x).astype(np.float64)


def striped(idx):
    return np.tile(idx.reshape(-1, 16).T, (8, 1)).astype(np.uint16)


def unstriped(offs):
    return offs[:16].T.reshape(-1).astype(np.int64)


E2M1 = np.array([0.0, 0.5, 1.0, 1.5, 2.0, 3.0, 4.0, 6.0, -0.0, -0.5, -1.0, -1.5, -2.0, -3.0, -4.0, -6.0])


def pack_weight(w, fmt):
    k, n = w.shape
    w = f64(np.asarray(w, np.float32).astype(ml_dtypes.bfloat16)).reshape(k // 32, 32, n)
    amax = np.abs(w).max(1)
    if fmt == "e4m3":
        byte = np.frexp(amax)[1] - 1 + 127 - 7
    else:
        mant, ex = np.frexp(amax / 6.0)
        byte = np.where(mant > 0.5, ex, ex - 1) + 127
    byte = np.clip(np.where(amax > 0, byte, 1), 1, 254)
    scaled = (w * np.exp2(127.0 - byte)[:, None, :]).reshape(k, n).astype(np.float32)
    by_word = np.ascontiguousarray(scaled.reshape(k // 512, 128, 4, n).transpose(0, 1, 3, 2))
    if fmt == "e4m3":
        words = by_word.astype(ml_dtypes.float8_e4m3fn).view(np.uint8)
    else:
        c = by_word.astype(ml_dtypes.float4_e2m1fn).view(np.uint8) & 0xF
        words = (c[..., 0::2] | (c[..., 1::2] << 4)).reshape(k // 512, 128, 2 * n)
    return np.ascontiguousarray(words), np.ascontiguousarray(byte.astype(np.uint8).reshape(k // 512, 16, n))


def unpack_weight(words, scales, fmt):
    g, _, n = scales.shape
    words = np.ascontiguousarray(words).reshape(g, 128, n, -1)
    if fmt == "e4m3":
        vals = words.view(ml_dtypes.float8_e4m3fn).astype(np.float64)
    else:
        nib = np.empty((g, 128, n, 4), np.uint8)
        nib[..., 0::2] = words & 0xF
        nib[..., 1::2] = words >> 4
        vals = E2M1[nib]
    vals = vals * np.repeat(np.exp2(scales.astype(np.float64) - 127.0), 8, axis=1)[..., None]
    return vals.transpose(0, 1, 3, 2).reshape(g * 512, n)


def gelu(v):
    return 0.5 * v * (1.0 + np.tanh(np.sqrt(2.0 / np.pi) * (v + 0.044715 * v**3)))


K, H, T, S = 512, 1024, 4096, 1024

def setup_inputs():
    n = np.random.standard_normal
    s = mx_kscale(K)[:, None]
    u = mx_kscale(H)[:, None]
    tab_words, tab_scales = pack_weight(n((K, T)) * s, "e2m1")
    w2_words, w2_scales = pack_weight(n((K, H)) / np.sqrt(K) / s / u.T, "e4m3")
    wk = np.eye(K) + 0.5 * n((K, K)) / np.sqrt(K)
    wk_words, wk_scales = pack_weight(wk / s / s.T, "e4m3")
    return {
        "tab_words": tab_words, "tab_scales": tab_scales,
        "offs": striped(np.random.permutation(T)[:S]),
        "offs2": striped(np.random.permutation(T)[:S]),
        "w1": (n((K, H)) / np.sqrt(K) / s / u.T).astype(np.float32),
        "w2_words": w2_words, "w2_scales": w2_scales,
        "wk_words": wk_words, "wk_scales": wk_scales,
        "cw": (np.exp(0.3 * n(H)) * u[:, 0] ** 2).astype(np.float32),
        "gn": (np.exp(0.3 * n(K)) * s[:, 0]).astype(np.float32),
    }

def reference(tab_words, tab_scales, offs, offs2, w1, w2_words, w2_scales, wk_words, wk_scales, cw, gn):
    TW = unpack_weight(tab_words, tab_scales, "e2m1")
    v = TW[:, unstriped(offs)]
    v2 = TW[:, unstriped(offs2)]
    w1q = mxq(f64(w1), 0, "e4m3")
    w2 = unpack_weight(w2_words, w2_scales, "e4m3")
    wk = unpack_weight(wk_words, wk_scales, "e4m3")
    d = (w1q.T @ v) - (w2.T @ v2)
    t = f64(cw)[:, None] * d
    h = t / (1.0 + t * d)
    hq = mxq(h, 0, "e4m3")
    w1r = mxq(f64(w1).T, 0, "e4m3")
    y = w1r.T @ hq + wk.T @ v
    return f64(gn)[:, None] * y

@@ -1,0 +1,299 @@
+from contextlib import ExitStack
+
+import concourse.mybir as mybir
+from concourse.masks import make_identity
+
+K, H, T, S = 512, 1024, 4096, 1024
+FLOPS = 2 * S * (2 * K * H + H * K + K * K)
+
+F32 = mybir.dt.float32
+BF16 = mybir.dt.bfloat16
+I32 = mybir.dt.int32
+U32 = mybir.dt.uint32
+U16 = mybir.dt.uint16
+U8 = mybir.dt.uint8
+FP8X4 = mybir.dt.float8_e4m3fn_x4
+FP4X4 = mybir.dt.float4_e2m1fn_x4
+ALU = mybir.AluOpType
+ACT = mybir.ActivationFunctionType
+
+P = 128
+BANK = 512
+HALF = 512
+CHUNKS = [512, 256, 256]
+P1_ENG = "vvvvvvvvvvvvvvvv"
+P3_ENG = "ssssssssssssssss"
+P5_ENG = "ssssssssssssssss"
+P6_ENG = "gggggv"
+OUT_ENG = "vvvvvvvvvsvs"
+
+
+def tile_list_segment_successor_refinement_kernel(
+    tc, tab_words, tab_scales, offs, offs2, w1, w2_words, w2_scales, wk_words, wk_scales, cw, gn, out
+):
+    nc = tc.nc
+    with ExitStack() as ctx:
+        keep = ctx.enter_context(tc.tile_pool(name="keep", bufs=1))
+        work = ctx.enter_context(tc.tile_pool(name="work", bufs=3))
+        psum = ctx.enter_context(tc.psum_pool(name="psum", bufs=2))
+
+        def kept(shape, dtype, name):
+            return keep.tile(shape, dtype, name=name, align_bytes=64)
+
+        lists = [keep.tile([P, S // 16], U16, name="list_a"), keep.tile([P, S // 16], U16, name="list_b")]
+        table_words = kept([P, T], U16, "table_words")
+        table_scales = kept([P, T], U8, "table_scales")
+        w1_raw = [kept([P, 4, 512], F32, "w1_raw%d" % b) for b in range(2)]
+        w2_words_raw = keep.tile([P, H], U32, name="w2_words_raw", tag="packed_weight", align_bytes=64)
+        w2_scales_raw = kept([P, H], U8, "w2_scales_raw")
+        wk_plane = kept([P, K], U8, "wk_plane")
+        vectors = kept([P, P], F32, "vectors")
+        ident = kept([P, P], F32, "ident")
+
+        nc.vector.memset(table_scales[:].bitcast(I32), 0)
+        nc.vector.memset(w2_scales_raw[:].bitcast(I32), 0)
+        nc.vector.memset(wk_plane[:].bitcast(I32), 0)
+        nc.gpsimd.memset(vectors[:], 0.0)
+        make_identity(nc, ident[:])
+
+        def load_scale_rows(queue, plane, rows):
+            for q in range(4):
+                queue.dma_start(out=plane[32 * q : 32 * q + 4, :].bitcast(I32), in_=rows[0, 4 * q : 4 * q + 4, :].bitcast(I32))
+
+        def load_w1(b):
+            nc.sync.dma_start(out=w1_raw[b][:], in_=w1[:, 512 * b : 512 * (b + 1)].rearrange("(p j) c -> p j c", j=4))
+
+        warm = kept([P, 2], F32, "warm")
+        nc.vector.memset(warm[:, 0:1], 1.0)
+        nc.sync.dma_start(lists[0][:], offs)
+        nc.sync.dma_start(out=table_words[:].bitcast(I32), in_=tab_words[0].bitcast(I32))
+        nc.sync.dma_start(lists[1][:], offs2)
+        load_w1(0)
+        nc.sync.dma_start(out=w2_words_raw[:].bitcast(I32), in_=w2_words[0].rearrange("p c i -> p (c i)").bitcast(I32))
+        load_w1(1)
+        load_scale_rows(nc.scalar, table_scales, tab_scales)
+        nc.scalar.activation(out=warm[:, 1:2], in_=warm[:, 0:1], func=ACT.Abs_reciprocal_sqrt)
+        load_scale_rows(nc.gpsimd, w2_scales_raw, w2_scales)
+        for b in range(2):
+            nc.gpsimd.dma_start(
+                out=vectors[4 * b : 4 * b + 4, :].rearrange("t (g i) -> t g i", i=8),
+                in_=cw[512 * b : 512 * (b + 1)].rearrange("(g t i) -> t g i", t=4, i=8),
+            )
+        nc.gpsimd.dma_start(out=vectors[8:12, :], in_=gn.rearrange("(c p) -> c p", p=P))
+        load_scale_rows(nc.gpsimd, wk_plane, wk_scales)
+
+        picked_words = [[kept([P, HALF], U16, "picked_words%d%d" % (a, h)) for h in range(2)] for a in range(2)]
+        picked_scales = [[kept([P, HALF], U8, "picked_scales%d%d" % (a, h)) for h in range(2)] for a in range(2)]
+
+        def gather_scales(h):
+            for a in range(2):
+                nc.vector.tensor_copy(picked_scales[a][h][:], table_scales[:].indirect(lists[a][:, 32 * h : 32 * (h + 1)]))
+
+        def gather_words(h):
+            for a in range(2):
+                nc.vector.tensor_copy(picked_words[a][h][:], table_words[:].indirect(lists[a][:, 32 * h : 32 * (h + 1)]))
+
+        w1k_bf16 = [kept([P, 2048], BF16, "w1k_bf16_%d" % b) for b in range(2)]
+        w1k_codes = [kept([P, 512], U32, "w1k_codes%d" % b) for b in range(2)]
+        w1k_plane = [kept([P, 512], U8, "w1k_plane%d" % b) for b in range(2)]
+        w1r_bf16 = [kept([P, 2048], BF16, "w1r_bf16_%d" % b) for b in range(2)]
+        w1r_codes = [kept([P, 512], U32, "w1r_codes%d" % b) for b in range(2)]
+        w1r_plane = [kept([P, 512], U8, "w1r_plane%d" % b) for b in range(2)]
+        w2_codes = kept([P, H], U32, "w2_codes")
+        w2_plane = kept([P, H], U8, "w2_plane")
+        inv_cw = kept([P, 8], F32, "inv_cw")
+        gain = kept([P, 4], F32, "gain")
+
+        def round_w1(b):
+            for t in range(4):
+                nc.scalar.copy(
+                    out=w1k_bf16[b][:, 512 * t : 512 * (t + 1)].rearrange("p (g x i j) -> p g x j i", g=16, x=2, i=4, j=4),
+                    in_=w1_raw[b][:].rearrange("p j (g t x i) -> p t g x j i", g=16, t=4, x=2, i=4)[:, t],
+                )
+
+        def quantise(codes, plane, values):
+            nc.vector.quantize_mx(out=codes.bitcast(FP8X4), scales=plane, in_=values)
+
+        def turn_w1(b):
+            words = w1k_bf16[b][:].bitcast(F32)
+            for u in range(2):
+                bank = psum.tile([P, 4, P], F32, name="sum_bank", tag="sum_bank", bufs=4)
+                for t in range(4):
+                    nc.tensor.transpose(bank[:, t, :], words[:, 256 * t + u : 256 * (t + 1) : 2], ident[:])
+                nc.scalar.copy(
+                    out=w1r_bf16[b][:].rearrange("m (p u e t) -> m u p e t", u=2, e=2, t=4)[:, u],
+                    in_=bank[:].rearrange("m t p -> m (t p)").bitcast(BF16).rearrange("m (t p e) -> m p e t", t=4, e=2),
+                )
+
+        def order_w2():
+            nc.vector.tensor_copy(
+                out=w2_codes[:].bitcast(I32).rearrange("p (b t g i) -> p b t g i", b=2, t=4, i=8),
+                in_=w2_words_raw[:].bitcast(I32).rearrange("p (b g t i) -> p b t g i", b=2, t=4, i=8),
+            )
+            nc.vector.tensor_copy(
+                out=w2_plane[:].bitcast(I32).rearrange("p (b t g i) -> p b t g i", b=2, t=4, i=2),
+                in_=w2_scales_raw[:].bitcast(I32).rearrange("p (b g t i) -> p b t g i", b=2, t=4, i=2),
+            )
+
+        def turn_vectors():
+            bank = psum.tile([P, 4, P], F32, name="sum_bank", tag="sum_bank", bufs=4)
+            nc.tensor.transpose(bank[:, 0, :], vectors[:], ident[:])
+            nc.vector.reciprocal(out=inv_cw[:], in_=bank[:, 0, 0:8])
+            nc.vector.tensor_copy(out=gain[:], in_=bank[:, 0, 8:12])
+
+        gather_words(0)
+        gather_words(1)
+        round_w1(0)
+        gather_scales(0)
+        quantise(w1k_codes[0][:], w1k_plane[0][:], w1k_bf16[0][:])
+        order_w2()
+        wk_codes = keep.tile([P, K], U32, name="wk_codes", tag="packed_weight", align_bytes=64)
+        nc.sync.dma_start(out=wk_codes[:].bitcast(I32), in_=wk_words[0].rearrange("p c i -> p (c i)").bitcast(I32))
+        turn_w1(0)
+        turn_vectors()
+        round_w1(1)
+        quantise(w1k_codes[1][:], w1k_plane[1][:], w1k_bf16[1][:])
+        turn_w1(1)
+
+        units = []
+        j0 = 0
+        for c, width in enumerate(CHUNKS):
+            per_bank = BANK // width
+            for b in range(2):
+                for t0 in range(0, 4, per_bank):
+                    units.append((c, j0, width, b, t0, per_bank))
+            j0 = j0 + width
+        state = {}
+
+        def moving(a, j0, width):
+            h, lo = divmod(j0, HALF)
+            return picked_words[a][h][:, lo : lo + width].bitcast(FP4X4), picked_scales[a][h][:, lo : lo + width]
+
+        def products(n):
+            c, j0, width, b, t0, per_bank = units[n]
+            own = psum.tile([P, per_bank, width], F32, name="own", tag="own")
+            nxt = psum.tile([P, per_bank, width], F32, name="nxt", tag="nxt")
+            for bank, codes, plane, base, a in ((nxt, w2_codes, w2_plane, 512 * b, 1), (own, w1k_codes[b], w1k_plane[b], 0, 0)):
+                rhs, rhs_scale = moving(a, j0, width)
+                for x in range(per_bank):
+                    cols = slice(base + P * (t0 + x), base + P * (t0 + x + 1))
+                    nc.tensor.matmul_mx(
+                        out=bank[:, x, :], lhsT=codes[:, cols].bitcast(FP8X4), lhsT_scale=plane[:, cols],
+                        rhs=rhs, rhs_scale=rhs_scale, start=True, stop=True,
+                    )
+            state[n, "own"] = own
+            state[n, "nxt"] = nxt
+            if t0 == 0:
+                for tag in ("d", "sq", "rs", "r2"):
+                    state[c, b, tag] = work.tile([P, 4 * width], F32, name=tag, tag=tag, bufs=3)
+
+        def part(n, tag):
+            c, j0, width, b, t0, per_bank = units[n]
+            return state[c, b, tag][:, t0 * width : (t0 + per_bank) * width]
+
+        def flat(bank):
+            return bank[:].rearrange("p x w -> p (x w)")
+
+        def leave(n):
+            succ = work.tile([P, BANK], F32, name="succ", tag="succ")
+            if P1_ENG[n] == "v":
+                nc.vector.tensor_copy(out=succ[:], in_=flat(state[n, "nxt"]))
+            else:
+                nc.scalar.copy(out=succ[:], in_=flat(state[n, "nxt"]))
+            state[n, "succ"] = succ
+
+        def subtract(n):
+            nc.vector.tensor_tensor(out=part(n, "d"), in0=flat(state[n, "own"]), in1=state[n, "succ"][:], op=ALU.subtract)
+
+        def square(eng, dst, src):
+            if eng == "s":
+                nc.scalar.activation(out=dst, in_=src, func=ACT.Square)
+            elif eng == "v":
+                nc.vector.tensor_tensor(out=dst, in0=src, in1=src, op=ALU.mult)
+            else:
+                nc.gpsimd.tensor_tensor(out=dst, in0=src, in1=src, op=ALU.mult)
+
+        def damp(n):
+            c, j0, width, b, t0, per_bank = units[n]
+            for t in range(t0, t0 + per_bank):
+                cols = slice(t * width, (t + 1) * width)
+                nc.scalar.activation(
+                    out=state[c, b, "rs"][:, cols], in_=state[c, b, "sq"][:, cols], func=ACT.Abs_reciprocal_sqrt,
+                    bias=inv_cw[:, 4 * b + t : 4 * b + t + 1],
+                )
+
+        def weave(n):
+            c, j0, width, b, t0, per_bank = units[n]
+            if t0 + per_bank < 4:
+                return
+            h_bf16 = work.tile([P, 4 * width], BF16, name="h_bf16", tag="h_bf16", bufs=2, align_bytes=64)
+            eng = nc.vector if P6_ENG[2 * c + b] == "v" else nc.gpsimd
+            for lo in range(0, width, 128):
+                hi = min(width, lo + 128)
+                eng.tensor_tensor(
+                    out=h_bf16[:, 4 * lo : 4 * hi].rearrange("p (c i t) -> p c t i", i=2, t=4),
+                    in0=state[c, b, "d"][:].rearrange("p (t c i) -> p c t i", t=4, i=2)[:, lo // 2 : hi // 2],
+                    in1=state[c, b, "r2"][:].rearrange("p (t c i) -> p c t i", t=4, i=2)[:, lo // 2 : hi // 2],
+                    op=ALU.mult,
+                )
+            state[c, b, "h"] = h_bf16
+
+        def back(n):
+            c, j0, width, b, t0, per_bank = units[n]
+            if t0 + per_bank < 4:
+                return
+            h_codes = work.tile([P, width], U32, name="h_codes", tag="h_codes", bufs=2, align_bytes=64)
+            h_plane = work.tile([P, width], U8, name="h_plane", tag="h_plane", bufs=2, align_bytes=64)
+            if c == 0:
+                quantise(w1r_codes[b][:], w1r_plane[b][:], w1r_bf16[b][:])
+            quantise(h_codes[:], h_plane[:], state[c, b, "h"][:])
+            for nt in range(4):
+                cols = slice(P * nt, P * (nt + 1))
+                if b == 0:
+                    y = psum.tile([P, width], F32, name="sum_bank", tag="sum_bank", bufs=4)
+                    state[c, nt, "y"] = y
+                y = state[c, nt, "y"]
+                nc.tensor.matmul_mx(
+                    out=y[:], lhsT=w1r_codes[b][:, cols].bitcast(FP8X4), lhsT_scale=w1r_plane[b][:, cols],
+                    rhs=h_codes[:].bitcast(FP8X4), rhs_scale=h_plane[:], start=(b == 0), stop=(b == 1),
+                )
+                if b == 0:
+                    step = BANK if width == BANK else P
+                    for lo in range(0, width, step):
+                        rhs, rhs_scale = moving(0, j0 + lo, step)
+                        nc.tensor.matmul_mx(
+                            out=y[:, lo : lo + step], lhsT=wk_codes[:, cols].bitcast(FP8X4), lhsT_scale=wk_plane[:, cols],
+                            rhs=rhs, rhs_scale=rhs_scale, start=False, stop=False,
+                        )
+
+        def finish(n):
+            c, j0, width, b, t0, per_bank = units[n]
+            if t0 + per_bank < 4 or b == 0:
+                return
+            for nt in range(4):
+                result = work.tile([P, width], F32, name="result", tag="result", bufs=4)
+                if OUT_ENG[4 * c + nt] == "v":
+                    nc.vector.tensor_scalar(
+                        out=result[:], in0=state[c, nt, "y"][:], scalar1=gain[:, nt : nt + 1], scalar2=None, op0=ALU.mult
+                    )
+                else:
+                    nc.scalar.activation(out=result[:], in_=state[c, nt, "y"][:], func=ACT.Copy, scale=gain[:, nt : nt + 1])
+                nc.sync.dma_start(out=out[P * nt : P * (nt + 1), j0 : j0 + width], in_=result[:])
+
+        stages = [
+            products,
+            leave,
+            subtract,
+            lambda n: square(P3_ENG[n], part(n, "sq"), part(n, "d")),
+            damp,
+            lambda n: square(P5_ENG[n], part(n, "r2"), part(n, "rs")),
+            weave,
+            back,
+            finish,
+        ]
+        for step in range(len(units) + len(stages) - 1):
+            for lag, stage in enumerate(stages):
+                if 0 <= step - lag < len(units):
+                    stage(step - lag)
+            if step == 2:
+                gather_scales(1)

@@ -20,12 +20,16 @@ ACT = mybir.ActivationFunctionType
 P = 128
 BANK = 512
 HALF = 512
-CHUNKS = [512, 256, 256]
-P1_ENG = "vvvvvvvvvvvvvvvv"
+CHUNKS = [512,256,256]
+P1_ENG = "ssssssvvvvvvvvvv"
 P3_ENG = "ssssssssssssssss"
 P5_ENG = "ssssssssssssssss"
-P6_ENG = "gggggv"
-OUT_ENG = "vvvvvvvvvsvs"
+P6_ENG = "vvvvvvvv"
+OUT_ENG = "vvvvvsvsvsvsvsvs"
+WIDE = "1122222222222211"
+PIECE = 128
+LAGS = [0,0,1,2,3,4,5,6,6,7,7,8]
+HOLD = [0,1,2,3]
 
 
 def tile_list_segment_successor_refinement_kernel(
@@ -41,38 +45,48 @@ def tile_list_segment_successor_refinement_kernel(
             return keep.tile(shape, dtype, name=name, align_bytes=64)
 
         lists = [keep.tile([P, S // 16], U16, name="list_a"), keep.tile([P, S // 16], U16, name="list_b")]
-        table_words = kept([P, T], U16, "table_words")
+        one = keep.tile([P, 1], F32, name="one", tag="first", align_bytes=64)
+        warm = keep.tile([P, 1], F32, name="warm", tag="second", align_bytes=64)
+        nought = keep.tile([P, 1], F32, name="nought", tag="third", align_bytes=64)
         table_scales = kept([P, T], U8, "table_scales")
-        w1_raw = [kept([P, 4, 512], F32, "w1_raw%d" % b) for b in range(2)]
-        w2_words_raw = keep.tile([P, H], U32, name="w2_words_raw", tag="packed_weight", align_bytes=64)
-        w2_scales_raw = kept([P, H], U8, "w2_scales_raw")
-        wk_plane = kept([P, K], U8, "wk_plane")
+        w1_first = kept([P, 4 * 512], F32, "w1_first")
+        w2_scales_raw = keep.tile([P, H], U8, name="w2_scales_raw", tag="weight_plane", align_bytes=64)
         vectors = kept([P, P], F32, "vectors")
         ident = kept([P, P], F32, "ident")
 
+        nc.vector.memset(one[:], 1.0)
+        nc.vector.memset(nought[:], 0.0)
         nc.vector.memset(table_scales[:].bitcast(I32), 0)
-        nc.vector.memset(w2_scales_raw[:].bitcast(I32), 0)
-        nc.vector.memset(wk_plane[:].bitcast(I32), 0)
-        nc.gpsimd.memset(vectors[:], 0.0)
+        nc.gpsimd.memset(w2_scales_raw[:].bitcast(I32), 0)
         make_identity(nc, ident[:])
+        nc.vector.memset(vectors[:], 0.0)
+        nc.scalar.activation(out=warm[:], in_=one[:], func=ACT.Abs_reciprocal_sqrt, bias=nought[:])
 
         def load_scale_rows(queue, plane, rows):
             for q in range(4):
                 queue.dma_start(out=plane[32 * q : 32 * q + 4, :].bitcast(I32), in_=rows[0, 4 * q : 4 * q + 4, :].bitcast(I32))
 
-        def load_w1(b):
-            nc.sync.dma_start(out=w1_raw[b][:], in_=w1[:, 512 * b : 512 * (b + 1)].rearrange("(p j) c -> p j c", j=4))
+        def load_w1(b, dst):
+            nc.sync.dma_start(out=dst.rearrange("p (j c) -> p j c", j=4), in_=w1[:, 512 * b : 512 * (b + 1)].rearrange("(p j) c -> p j c", j=4))
 
-        warm = kept([P, 2], F32, "warm")
-        nc.vector.memset(warm[:, 0:1], 1.0)
         nc.sync.dma_start(lists[0][:], offs)
-        nc.sync.dma_start(out=table_words[:].bitcast(I32), in_=tab_words[0].bitcast(I32))
         nc.sync.dma_start(lists[1][:], offs2)
-        load_w1(0)
-        nc.sync.dma_start(out=w2_words_raw[:].bitcast(I32), in_=w2_words[0].rearrange("p c i -> p (c i)").bitcast(I32))
-        load_w1(1)
-        load_scale_rows(nc.scalar, table_scales, tab_scales)
-        nc.scalar.activation(out=warm[:, 1:2], in_=warm[:, 0:1], func=ACT.Abs_reciprocal_sqrt)
+        load_w1(0, w1_first[:])
+        load_scale_rows(nc.sync, table_scales, tab_scales)
+        table_words = keep.tile([P, T], U16, name="table_words", tag="first", align_bytes=64)
+        nc.sync.dma_start(out=table_words[:].bitcast(I32), in_=tab_words[0].bitcast(I32))
+        w2_words_hbm = w2_words[0].rearrange("p c i -> p (c i)").bitcast(I32)
+        w2_words_raw = []
+
+        def load_w2_words(b):
+            raw = keep.tile([P, 512], I32, name="w2_words_raw%d" % b, tag="third", align_bytes=64)
+            nc.sync.dma_start(out=raw[:], in_=w2_words_hbm[:, 512 * b : 512 * (b + 1)])
+            w2_words_raw.append(raw)
+
+        load_w2_words(0)
+        w1_second = keep.tile([P, 4 * 512], F32, name="w1_second", tag="second", align_bytes=64)
+        load_w1(1, w1_second[:])
+        w1_raw = [w1_first[:], w1_second[:]]
         load_scale_rows(nc.gpsimd, w2_scales_raw, w2_scales)
         for b in range(2):
             nc.gpsimd.dma_start(
@@ -80,18 +94,16 @@ def tile_list_segment_successor_refinement_kernel(
                 in_=cw[512 * b : 512 * (b + 1)].rearrange("(g t i) -> t g i", t=4, i=8),
             )
         nc.gpsimd.dma_start(out=vectors[8:12, :], in_=gn.rearrange("(c p) -> c p", p=P))
-        load_scale_rows(nc.gpsimd, wk_plane, wk_scales)
 
-        picked_words = [[kept([P, HALF], U16, "picked_words%d%d" % (a, h)) for h in range(2)] for a in range(2)]
-        picked_scales = [[kept([P, HALF], U8, "picked_scales%d%d" % (a, h)) for h in range(2)] for a in range(2)]
+        picked_words = [[], []]
+        picked_scales = [[], []]
 
-        def gather_scales(h):
-            for a in range(2):
-                nc.vector.tensor_copy(picked_scales[a][h][:], table_scales[:].indirect(lists[a][:, 32 * h : 32 * (h + 1)]))
-
-        def gather_words(h):
-            for a in range(2):
-                nc.vector.tensor_copy(picked_words[a][h][:], table_words[:].indirect(lists[a][:, 32 * h : 32 * (h + 1)]))
+        def gather(kind, a, h):
+            table, picked, dtype = ((table_scales, picked_scales, U8), (table_words, picked_words, U16))[kind]
+            name = "picked%d%d%d" % (kind, a, h)
+            dst = keep.tile([P, HALF], dtype, name=name, tag=("early%d" % (2 * kind + a) if h else name), align_bytes=64)
+            nc.vector.tensor_copy(dst[:], table[:].indirect(lists[a][:, 32 * h : 32 * (h + 1)]))
+            picked[a].append(dst)
 
         w1k_bf16 = [kept([P, 2048], BF16, "w1k_bf16_%d" % b) for b in range(2)]
         w1k_codes = [kept([P, 512], U32, "w1k_codes%d" % b) for b in range(2)]
@@ -108,7 +120,7 @@ def tile_list_segment_successor_refinement_kernel(
             for t in range(4):
                 nc.scalar.copy(
                     out=w1k_bf16[b][:, 512 * t : 512 * (t + 1)].rearrange("p (g x i j) -> p g x j i", g=16, x=2, i=4, j=4),
-                    in_=w1_raw[b][:].rearrange("p j (g t x i) -> p t g x j i", g=16, t=4, x=2, i=4)[:, t],
+                    in_=w1_raw[b].rearrange("p (j g t x i) -> p t g x j i", j=4, g=16, t=4, x=2, i=4)[:, t],
                 )
 
         def quantise(codes, plane, values):
@@ -125,11 +137,14 @@ def tile_list_segment_successor_refinement_kernel(
                     in_=bank[:].rearrange("m t p -> m (t p)").bitcast(BF16).rearrange("m (t p e) -> m p e t", t=4, e=2),
                 )
 
-        def order_w2():
+        def order_w2_words(b):
             nc.vector.tensor_copy(
-                out=w2_codes[:].bitcast(I32).rearrange("p (b t g i) -> p b t g i", b=2, t=4, i=8),
-                in_=w2_words_raw[:].bitcast(I32).rearrange("p (b g t i) -> p b t g i", b=2, t=4, i=8),
+                out=w2_codes[:, 512 * b : 512 * (b + 1)].bitcast(I32).rearrange("p (t g i) -> p t g i", t=4, i=8),
+                in_=w2_words_raw[b][:].rearrange("p (g t i) -> p t g i", t=4, i=8),
             )
+
+        def order_w2():
+            order_w2_words(0)
             nc.vector.tensor_copy(
                 out=w2_plane[:].bitcast(I32).rearrange("p (b t g i) -> p b t g i", b=2, t=4, i=2),
                 in_=w2_scales_raw[:].bitcast(I32).rearrange("p (b g t i) -> p b t g i", b=2, t=4, i=2),
@@ -141,19 +156,25 @@ def tile_list_segment_successor_refinement_kernel(
             nc.vector.reciprocal(out=inv_cw[:], in_=bank[:, 0, 0:8])
             nc.vector.tensor_copy(out=gain[:], in_=bank[:, 0, 8:12])
 
-        gather_words(0)
-        gather_words(1)
         round_w1(0)
-        gather_scales(0)
+        turn_w1(0)
+        gather(0, 1, 0)
+        gather(0, 0, 0)
+        gather(1, 1, 0)
+        gather(1, 0, 0)
         quantise(w1k_codes[0][:], w1k_plane[0][:], w1k_bf16[0][:])
         order_w2()
-        wk_codes = keep.tile([P, K], U32, name="wk_codes", tag="packed_weight", align_bytes=64)
-        nc.sync.dma_start(out=wk_codes[:].bitcast(I32), in_=wk_words[0].rearrange("p c i -> p (c i)").bitcast(I32))
-        turn_w1(0)
+        load_w2_words(1)
         turn_vectors()
         round_w1(1)
-        quantise(w1k_codes[1][:], w1k_plane[1][:], w1k_bf16[1][:])
         turn_w1(1)
+        wk_plane = keep.tile([P, K], U8, name="wk_plane", tag="weight_plane", align_bytes=64)
+        wk_codes = keep.tile([P, K], U32, name="wk_codes", tag="w1_first", align_bytes=64)
+
+        def load_wk():
+            nc.gpsimd.memset(wk_plane[:].bitcast(I32), 0)
+            load_scale_rows(nc.sync, wk_plane, wk_scales)
+            nc.sync.dma_start(out=wk_codes[:].bitcast(I32), in_=wk_words[0].rearrange("p c i -> p (c i)").bitcast(I32))
 
         units = []
         j0 = 0
@@ -185,7 +206,7 @@ def tile_list_segment_successor_refinement_kernel(
             state[n, "nxt"] = nxt
             if t0 == 0:
                 for tag in ("d", "sq", "rs", "r2"):
-                    state[c, b, tag] = work.tile([P, 4 * width], F32, name=tag, tag=tag, bufs=3)
+                    state[c, b, tag] = work.tile([P, 4 * width], F32, name=tag, tag=tag, bufs=4)
 
         def part(n, tag):
             c, j0, width, b, t0, per_bank = units[n]
@@ -195,7 +216,10 @@ def tile_list_segment_successor_refinement_kernel(
             return bank[:].rearrange("p x w -> p (x w)")
 
         def leave(n):
-            succ = work.tile([P, BANK], F32, name="succ", tag="succ")
+            if n in HOLD:
+                succ = keep.tile([P, BANK], F32, name="succ", tag="early%d" % HOLD.index(n), align_bytes=64)
+            else:
+                succ = work.tile([P, BANK], F32, name="succ", tag="succ", bufs=4)
             if P1_ENG[n] == "v":
                 nc.vector.tensor_copy(out=succ[:], in_=flat(state[n, "nxt"]))
             else:
@@ -228,8 +252,9 @@ def tile_list_segment_successor_refinement_kernel(
                 return
             h_bf16 = work.tile([P, 4 * width], BF16, name="h_bf16", tag="h_bf16", bufs=2, align_bytes=64)
             eng = nc.vector if P6_ENG[2 * c + b] == "v" else nc.gpsimd
-            for lo in range(0, width, 128):
-                hi = min(width, lo + 128)
+            step = PIECE if P6_ENG[2 * c + b] == "g" else 256
+            for lo in range(0, width, step):
+                hi = min(width, lo + step)
                 eng.tensor_tensor(
                     out=h_bf16[:, 4 * lo : 4 * hi].rearrange("p (c i t) -> p c t i", i=2, t=4),
                     in0=state[c, b, "d"][:].rearrange("p (t c i) -> p c t i", t=4, i=2)[:, lo // 2 : hi // 2],
@@ -242,58 +267,95 @@ def tile_list_segment_successor_refinement_kernel(
             c, j0, width, b, t0, per_bank = units[n]
             if t0 + per_bank < 4:
                 return
-            h_codes = work.tile([P, width], U32, name="h_codes", tag="h_codes", bufs=2, align_bytes=64)
-            h_plane = work.tile([P, width], U8, name="h_plane", tag="h_plane", bufs=2, align_bytes=64)
+            h_codes = work.tile([P, width], U32, name="h_codes", tag="h_codes", bufs=3, align_bytes=64)
+            h_plane = work.tile([P, width], U8, name="h_plane", tag="h_plane", bufs=3, align_bytes=64)
             if c == 0:
                 quantise(w1r_codes[b][:], w1r_plane[b][:], w1r_bf16[b][:])
             quantise(h_codes[:], h_plane[:], state[c, b, "h"][:])
-            for nt in range(4):
-                cols = slice(P * nt, P * (nt + 1))
-                if b == 0:
-                    y = psum.tile([P, width], F32, name="sum_bank", tag="sum_bank", bufs=4)
-                    state[c, nt, "y"] = y
-                y = state[c, nt, "y"]
-                nc.tensor.matmul_mx(
-                    out=y[:], lhsT=w1r_codes[b][:, cols].bitcast(FP8X4), lhsT_scale=w1r_plane[b][:, cols],
-                    rhs=h_codes[:].bitcast(FP8X4), rhs_scale=h_plane[:], start=(b == 0), stop=(b == 1),
-                )
-                if b == 0:
-                    step = BANK if width == BANK else P
-                    for lo in range(0, width, step):
-                        rhs, rhs_scale = moving(0, j0 + lo, step)
-                        nc.tensor.matmul_mx(
-                            out=y[:, lo : lo + step], lhsT=wk_codes[:, cols].bitcast(FP8X4), lhsT_scale=wk_plane[:, cols],
-                            rhs=rhs, rhs_scale=rhs_scale, start=False, stop=False,
-                        )
+            state[c, b, "hq"] = (h_codes, h_plane)
 
-        def finish(n):
+        def passes(c, j0, width, bb, nt):
+            cols = slice(P * nt, P * (nt + 1))
+            if bb == 0:
+                state[c, nt, "y"] = psum.tile([P, width], F32, name="sum_bank", tag="sum_bank", bufs=4)
+            y = state[c, nt, "y"]
+            codes, plane = state[c, bb, "hq"]
+            nc.tensor.matmul_mx(
+                out=y[:], lhsT=w1r_codes[bb][:, cols].bitcast(FP8X4), lhsT_scale=w1r_plane[bb][:, cols],
+                rhs=codes[:].bitcast(FP8X4), rhs_scale=plane[:], start=(bb == 0), stop=(bb == 1),
+            )
+            if bb == 0:
+                step = BANK if width == BANK else P
+                for lo in range(0, width, step):
+                    rhs, rhs_scale = moving(0, j0 + lo, step)
+                    nc.tensor.matmul_mx(
+                        out=y[:, lo : lo + step], lhsT=wk_codes[:, cols].bitcast(FP8X4), lhsT_scale=wk_plane[:, cols],
+                        rhs=rhs, rhs_scale=rhs_scale, start=False, stop=False,
+                    )
+
+        def finish(c, j0, width, nt):
+            result = work.tile([P, width], F32, name="result", tag="result", bufs=4)
+            if OUT_ENG[4 * c + nt] == "v":
+                nc.vector.tensor_scalar(
+                    out=result[:], in0=state[c, nt, "y"][:], scalar1=gain[:, nt : nt + 1], scalar2=None, op0=ALU.mult
+                )
+            else:
+                nc.scalar.activation(out=result[:], in_=state[c, nt, "y"][:], func=ACT.Copy, scale=gain[:, nt : nt + 1])
+            nc.sync.dma_start(out=out[P * nt : P * (nt + 1), j0 : j0 + width], in_=result[:])
+
+        def span(n, tag, count):
+            c, j0, width, b, t0, per_bank = units[n]
+            return state[c, b, tag][:, (t0 + per_bank - count * per_bank) * width : (t0 + per_bank) * width]
+
+        def wide_square(n, engines, dst, src):
+            if WIDE[n] == "1":
+                square(engines[n], span(n, dst, 1), span(n, src, 1))
+            elif n % 2 == 1:
+                square(engines[n], span(n, dst, 2), span(n, src, 2))
+
+        def wide_damp(n):
+            if WIDE[n] == "1":
+                damp(n)
+            elif n % 2 == 1:
+                damp(n - 1)
+                damp(n)
+
+        def second_product(n, part_no):
+            c, j0, width, b, t0, per_bank = units[n]
+            if t0 + per_bank < 4:
+                return
+            for nt in range(2 * part_no, 2 * part_no + 2):
+                passes(c, j0, width, b, nt)
+
+        def results(n, part_no):
             c, j0, width, b, t0, per_bank = units[n]
             if t0 + per_bank < 4 or b == 0:
                 return
-            for nt in range(4):
-                result = work.tile([P, width], F32, name="result", tag="result", bufs=4)
-                if OUT_ENG[4 * c + nt] == "v":
-                    nc.vector.tensor_scalar(
-                        out=result[:], in0=state[c, nt, "y"][:], scalar1=gain[:, nt : nt + 1], scalar2=None, op0=ALU.mult
-                    )
-                else:
-                    nc.scalar.activation(out=result[:], in_=state[c, nt, "y"][:], func=ACT.Copy, scale=gain[:, nt : nt + 1])
-                nc.sync.dma_start(out=out[P * nt : P * (nt + 1), j0 : j0 + width], in_=result[:])
+            for nt in range(2 * part_no, 2 * part_no + 2):
+                finish(c, j0, width, nt)
 
         stages = [
             products,
             leave,
             subtract,
-            lambda n: square(P3_ENG[n], part(n, "sq"), part(n, "d")),
-            damp,
-            lambda n: square(P5_ENG[n], part(n, "r2"), part(n, "rs")),
+            lambda n: wide_square(n, P3_ENG, "sq", "d"),
+            wide_damp,
+            lambda n: wide_square(n, P5_ENG, "r2", "rs"),
             weave,
             back,
-            finish,
+            lambda n: second_product(n, 0),
+            lambda n: second_product(n, 1),
+            lambda n: results(n, 0),
+            lambda n: results(n, 1),
         ]
-        for step in range(len(units) + len(stages) - 1):
-            for lag, stage in enumerate(stages):
+        for step in range(len(units) + max(LAGS)):
+            if step == 2:
+                order_w2_words(1)
+                quantise(w1k_codes[1][:], w1k_plane[1][:], w1k_bf16[1][:])
+            for lag, stage in zip(LAGS, stages):
                 if 0 <= step - lag < len(units):
                     stage(step - lag)
-            if step == 2:
-                gather_scales(1)
+            if step == 1:
+                load_wk()
+            if step - LAGS[2] in HOLD:
+                gather(HOLD.index(step - LAGS[2]) // 2, HOLD.index(step - LAGS[2]) % 2, 1)

@@ -21,15 +21,16 @@ P = 128
 BANK = 512
 HALF = 512
 CHUNKS = [512,256,256]
-P1_ENG = "ssssssvvvvvvvvvv"
+P1_ENG = "sssssvvvvvvvvvvv"
 P3_ENG = "ssssssssssssssss"
 P5_ENG = "ssssssssssssssss"
 P6_ENG = "vvvvvvvv"
 OUT_ENG = "vvvvvsvsvsvsvsvs"
-WIDE = "1122222222222211"
+WIDE = "2222222222222211"
 PIECE = 128
-LAGS = [0,0,1,2,3,4,5,6,6,7,7,8]
-HOLD = [0,1,2,3]
+LAGS = [0,1,2,3,4,5,6,7,8,9,9,10]
+RUN = 4
+HOLD = [0,2]
 
 
 def tile_list_segment_successor_refinement_kernel(
@@ -45,55 +46,52 @@ def tile_list_segment_successor_refinement_kernel(
             return keep.tile(shape, dtype, name=name, align_bytes=64)
 
         lists = [keep.tile([P, S // 16], U16, name="list_a"), keep.tile([P, S // 16], U16, name="list_b")]
-        one = keep.tile([P, 1], F32, name="one", tag="first", align_bytes=64)
-        warm = keep.tile([P, 1], F32, name="warm", tag="second", align_bytes=64)
-        nought = keep.tile([P, 1], F32, name="nought", tag="third", align_bytes=64)
+        warm = kept([P, 16], F32, "warm")
         table_scales = kept([P, T], U8, "table_scales")
         w1_first = kept([P, 4 * 512], F32, "w1_first")
-        w2_scales_raw = keep.tile([P, H], U8, name="w2_scales_raw", tag="weight_plane", align_bytes=64)
-        vectors = kept([P, P], F32, "vectors")
         ident = kept([P, P], F32, "ident")
 
-        nc.vector.memset(one[:], 1.0)
-        nc.vector.memset(nought[:], 0.0)
         nc.vector.memset(table_scales[:].bitcast(I32), 0)
-        nc.gpsimd.memset(w2_scales_raw[:].bitcast(I32), 0)
-        make_identity(nc, ident[:])
+        nc.vector.memset(warm[:, 0:1], 1.0)
+        vectors = kept([P, P], F32, "vectors")
         nc.vector.memset(vectors[:], 0.0)
-        nc.scalar.activation(out=warm[:], in_=one[:], func=ACT.Abs_reciprocal_sqrt, bias=nought[:])
+        w2_scales_raw = kept([P, H // 4], I32, "w2_scales_raw")[:]
+        nc.gpsimd.memset(w2_scales_raw, 0)
+        make_identity(nc, ident[:])
+        nc.scalar.activation(out=warm[:, 8:9], in_=warm[:, 0:1], func=ACT.Abs_reciprocal_sqrt)
 
         def load_scale_rows(queue, plane, rows):
             for q in range(4):
-                queue.dma_start(out=plane[32 * q : 32 * q + 4, :].bitcast(I32), in_=rows[0, 4 * q : 4 * q + 4, :].bitcast(I32))
+                queue.dma_start(out=plane[32 * q : 32 * q + 4, :], in_=rows[0, 4 * q : 4 * q + 4, :].bitcast(I32))
 
         def load_w1(b, dst):
             nc.sync.dma_start(out=dst.rearrange("p (j c) -> p j c", j=4), in_=w1[:, 512 * b : 512 * (b + 1)].rearrange("(p j) c -> p j c", j=4))
 
+        table_words = kept([P, T], U16, "table_words")
+        w2_words_hbm = w2_words[0].rearrange("p c i -> p (c i)").bitcast(I32)
+        w2_first = keep.tile([P, 512], I32, name="w2_first", tag="third", align_bytes=64)
+        w2_words_raw = [w2_first[:, 0:512]]
+        w1_second = keep.tile([P, 4 * 512], F32, name="w1_second", tag="second", align_bytes=64)
+        w1_raw = [w1_first[:], w1_second[:]]
         nc.sync.dma_start(lists[0][:], offs)
+        nc.sync.dma_start(out=table_words[:].bitcast(I32), in_=tab_words[0].bitcast(I32))
         nc.sync.dma_start(lists[1][:], offs2)
         load_w1(0, w1_first[:])
-        load_scale_rows(nc.sync, table_scales, tab_scales)
-        table_words = keep.tile([P, T], U16, name="table_words", tag="first", align_bytes=64)
-        nc.sync.dma_start(out=table_words[:].bitcast(I32), in_=tab_words[0].bitcast(I32))
-        w2_words_hbm = w2_words[0].rearrange("p c i -> p (c i)").bitcast(I32)
-        w2_words_raw = []
-
-        def load_w2_words(b):
-            raw = keep.tile([P, 512], I32, name="w2_words_raw%d" % b, tag="third", align_bytes=64)
-            nc.sync.dma_start(out=raw[:], in_=w2_words_hbm[:, 512 * b : 512 * (b + 1)])
-            w2_words_raw.append(raw)
-
-        load_w2_words(0)
-        w1_second = keep.tile([P, 4 * 512], F32, name="w1_second", tag="second", align_bytes=64)
+        nc.sync.dma_start(out=w2_words_raw[0], in_=w2_words_hbm[:, 0:512])
         load_w1(1, w1_second[:])
-        w1_raw = [w1_first[:], w1_second[:]]
-        load_scale_rows(nc.gpsimd, w2_scales_raw, w2_scales)
+        load_scale_rows(nc.sync, table_scales[:].bitcast(I32), tab_scales)
         for b in range(2):
-            nc.gpsimd.dma_start(
+            nc.sync.dma_start(
                 out=vectors[4 * b : 4 * b + 4, :].rearrange("t (g i) -> t g i", i=8),
                 in_=cw[512 * b : 512 * (b + 1)].rearrange("(g t i) -> t g i", t=4, i=8),
             )
-        nc.gpsimd.dma_start(out=vectors[8:12, :], in_=gn.rearrange("(c p) -> c p", p=P))
+        nc.sync.dma_start(out=vectors[8:12, :], in_=gn.rearrange("(c p) -> c p", p=P))
+        load_scale_rows(nc.gpsimd, w2_scales_raw, w2_scales)
+
+        def load_w2_second():
+            raw = keep.tile([P, 512], I32, name="w2_second", tag="third", align_bytes=64)
+            nc.sync.dma_start(out=raw[:], in_=w2_words_hbm[:, 512:1024])
+            w2_words_raw.append(raw[:])
 
         picked_words = [[], []]
         picked_scales = [[], []]
@@ -101,7 +99,7 @@ def tile_list_segment_successor_refinement_kernel(
         def gather(kind, a, h):
             table, picked, dtype = ((table_scales, picked_scales, U8), (table_words, picked_words, U16))[kind]
             name = "picked%d%d%d" % (kind, a, h)
-            dst = keep.tile([P, HALF], dtype, name=name, tag=("early%d" % (2 * kind + a) if h else name), align_bytes=64)
+            dst = keep.tile([P, HALF], dtype, name=name, tag=("early%d" % a if h and kind == 0 else name), align_bytes=64)
             nc.vector.tensor_copy(dst[:], table[:].indirect(lists[a][:, 32 * h : 32 * (h + 1)]))
             picked[a].append(dst)
 
@@ -112,9 +110,7 @@ def tile_list_segment_successor_refinement_kernel(
         w1r_codes = [kept([P, 512], U32, "w1r_codes%d" % b) for b in range(2)]
         w1r_plane = [kept([P, 512], U8, "w1r_plane%d" % b) for b in range(2)]
         w2_codes = kept([P, H], U32, "w2_codes")
-        w2_plane = kept([P, H], U8, "w2_plane")
-        inv_cw = kept([P, 8], F32, "inv_cw")
-        gain = kept([P, 4], F32, "gain")
+        w2_plane = keep.tile([P, H], U8, name="w2_plane", tag="w1_first", align_bytes=64)
 
         def round_w1(b):
             for t in range(4):
@@ -140,40 +136,44 @@ def tile_list_segment_successor_refinement_kernel(
         def order_w2_words(b):
             nc.vector.tensor_copy(
                 out=w2_codes[:, 512 * b : 512 * (b + 1)].bitcast(I32).rearrange("p (t g i) -> p t g i", t=4, i=8),
-                in_=w2_words_raw[b][:].rearrange("p (g t i) -> p t g i", t=4, i=8),
+                in_=w2_words_raw[b].rearrange("p (g t i) -> p t g i", t=4, i=8),
             )
 
         def order_w2():
             order_w2_words(0)
             nc.vector.tensor_copy(
                 out=w2_plane[:].bitcast(I32).rearrange("p (b t g i) -> p b t g i", b=2, t=4, i=2),
-                in_=w2_scales_raw[:].bitcast(I32).rearrange("p (b g t i) -> p b t g i", b=2, t=4, i=2),
+                in_=w2_scales_raw.rearrange("p (b g t i) -> p b t g i", b=2, t=4, i=2),
             )
 
         def turn_vectors():
             bank = psum.tile([P, 4, P], F32, name="sum_bank", tag="sum_bank", bufs=4)
             nc.tensor.transpose(bank[:, 0, :], vectors[:], ident[:])
-            nc.vector.reciprocal(out=inv_cw[:], in_=bank[:, 0, 0:8])
-            nc.vector.tensor_copy(out=gain[:], in_=bank[:, 0, 8:12])
+            nc.vector.reciprocal(out=inv_cw, in_=bank[:, 0, 0:8])
+            nc.vector.tensor_copy(out=gain, in_=bank[:, 0, 8:12])
 
         round_w1(0)
         turn_w1(0)
-        gather(0, 1, 0)
+        for h in range(2):
+            for a in range(2):
+                gather(1, a, h)
         gather(0, 0, 0)
-        gather(1, 1, 0)
-        gather(1, 0, 0)
         quantise(w1k_codes[0][:], w1k_plane[0][:], w1k_bf16[0][:])
+        gather(0, 1, 0)
         order_w2()
-        load_w2_words(1)
-        turn_vectors()
+        load_w2_second()
+        per_row = keep.tile([P, 12], F32, name="per_row", tag="w1k_bf16_0", align_bytes=64)
+        inv_cw = per_row[:, 0:8]
+        gain = per_row[:, 8:12]
         round_w1(1)
+        turn_vectors()
         turn_w1(1)
-        wk_plane = keep.tile([P, K], U8, name="wk_plane", tag="weight_plane", align_bytes=64)
-        wk_codes = keep.tile([P, K], U32, name="wk_codes", tag="w1_first", align_bytes=64)
+        wk_plane = keep.tile([P, K], U8, name="wk_plane", tag="third", align_bytes=64)
+        wk_codes = keep.tile([P, K], U32, name="wk_codes", tag="vectors", align_bytes=64)
 
         def load_wk():
-            nc.gpsimd.memset(wk_plane[:].bitcast(I32), 0)
-            load_scale_rows(nc.sync, wk_plane, wk_scales)
+            nc.vector.memset(wk_plane[:].bitcast(I32), 0)
+            load_scale_rows(nc.sync, wk_plane[:].bitcast(I32), wk_scales)
             nc.sync.dma_start(out=wk_codes[:].bitcast(I32), in_=wk_words[0].rearrange("p c i -> p (c i)").bitcast(I32))
 
         units = []
@@ -194,7 +194,7 @@ def tile_list_segment_successor_refinement_kernel(
             c, j0, width, b, t0, per_bank = units[n]
             own = psum.tile([P, per_bank, width], F32, name="own", tag="own")
             nxt = psum.tile([P, per_bank, width], F32, name="nxt", tag="nxt")
-            for bank, codes, plane, base, a in ((nxt, w2_codes, w2_plane, 512 * b, 1), (own, w1k_codes[b], w1k_plane[b], 0, 0)):
+            for bank, codes, plane, base, a in ((own, w1k_codes[b], w1k_plane[b], 0, 0), (nxt, w2_codes, w2_plane, 512 * b, 1)):
                 rhs, rhs_scale = moving(a, j0, width)
                 for x in range(per_bank):
                     cols = slice(base + P * (t0 + x), base + P * (t0 + x + 1))
@@ -206,7 +206,10 @@ def tile_list_segment_successor_refinement_kernel(
             state[n, "nxt"] = nxt
             if t0 == 0:
                 for tag in ("d", "sq", "rs", "r2"):
-                    state[c, b, tag] = work.tile([P, 4 * width], F32, name=tag, tag=tag, bufs=4)
+                    if n == 0 and tag == "sq":
+                        state[c, b, tag] = keep.tile([P, 4 * width], F32, name=tag, tag="second", align_bytes=64)
+                    else:
+                        state[c, b, tag] = work.tile([P, 4 * width], F32, name=tag, tag=tag, bufs=4)
 
         def part(n, tag):
             c, j0, width, b, t0, per_bank = units[n]
@@ -221,13 +224,13 @@ def tile_list_segment_successor_refinement_kernel(
             else:
                 succ = work.tile([P, BANK], F32, name="succ", tag="succ", bufs=4)
             if P1_ENG[n] == "v":
-                nc.vector.tensor_copy(out=succ[:], in_=flat(state[n, "nxt"]))
+                nc.vector.tensor_copy(out=succ[:], in_=flat(state[n, "own"]))
             else:
-                nc.scalar.copy(out=succ[:], in_=flat(state[n, "nxt"]))
+                nc.scalar.copy(out=succ[:], in_=flat(state[n, "own"]))
             state[n, "succ"] = succ
 
         def subtract(n):
-            nc.vector.tensor_tensor(out=part(n, "d"), in0=flat(state[n, "own"]), in1=state[n, "succ"][:], op=ALU.subtract)
+            nc.vector.tensor_tensor(out=part(n, "d"), in0=state[n, "succ"][:], in1=flat(state[n, "nxt"]), op=ALU.subtract)
 
         def square(eng, dst, src):
             if eng == "s":
@@ -252,13 +255,14 @@ def tile_list_segment_successor_refinement_kernel(
                 return
             h_bf16 = work.tile([P, 4 * width], BF16, name="h_bf16", tag="h_bf16", bufs=2, align_bytes=64)
             eng = nc.vector if P6_ENG[2 * c + b] == "v" else nc.gpsimd
+            run = RUN if P6_ENG[2 * c + b] == "g" else 2
             step = PIECE if P6_ENG[2 * c + b] == "g" else 256
             for lo in range(0, width, step):
                 hi = min(width, lo + step)
                 eng.tensor_tensor(
-                    out=h_bf16[:, 4 * lo : 4 * hi].rearrange("p (c i t) -> p c t i", i=2, t=4),
-                    in0=state[c, b, "d"][:].rearrange("p (t c i) -> p c t i", t=4, i=2)[:, lo // 2 : hi // 2],
-                    in1=state[c, b, "r2"][:].rearrange("p (t c i) -> p c t i", t=4, i=2)[:, lo // 2 : hi // 2],
+                    out=h_bf16[:, 4 * lo : 4 * hi].rearrange("p (c i t) -> p c t i", i=run, t=4),
+                    in0=state[c, b, "d"][:].rearrange("p (t c i) -> p c t i", t=4, i=run)[:, lo // run : hi // run],
+                    in1=state[c, b, "r2"][:].rearrange("p (t c i) -> p c t i", t=4, i=run)[:, lo // run : hi // run],
                     op=ALU.mult,
                 )
             state[c, b, "h"] = h_bf16
@@ -351,11 +355,10 @@ def tile_list_segment_successor_refinement_kernel(
         for step in range(len(units) + max(LAGS)):
             if step == 2:
                 order_w2_words(1)
+                load_wk()
                 quantise(w1k_codes[1][:], w1k_plane[1][:], w1k_bf16[1][:])
             for lag, stage in zip(LAGS, stages):
                 if 0 <= step - lag < len(units):
                     stage(step - lag)
-            if step == 1:
-                load_wk()
             if step - LAGS[2] in HOLD:
                 gather(HOLD.index(step - LAGS[2]) // 2, HOLD.index(step - LAGS[2]) % 2, 1)

@@ -18,19 +18,15 @@ ALU = mybir.AluOpType
 ACT = mybir.ActivationFunctionType
 
 P = 128
+PACK = 4
+K_PASS = P * PACK
 BANK = 512
-HALF = 512
-CHUNKS = [512,256,256]
-P1_ENG = "sssssvvvvvvvvvvv"
-P3_ENG = "ssssssssssssssss"
-P5_ENG = "ssssssssssssssss"
-P6_ENG = "vvvvvvvv"
-OUT_ENG = "vvvvvsvsvsvsvsvs"
-WIDE = "2222222222222211"
-PIECE = 128
-LAGS = [0,1,2,3,4,5,6,7,8,9,9,10]
-RUN = 4
-HOLD = [0,2]
+HALF = S // 2
+CHUNKS = [512, 256, 256]
+SCALAR_UNITS = 5
+LEAD = 3
+WEAVE = 256
+OWN, NEXT = 0, 1
 
 
 def tile_list_segment_successor_refinement_kernel(
@@ -39,326 +35,306 @@ def tile_list_segment_successor_refinement_kernel(
     nc = tc.nc
     with ExitStack() as ctx:
         keep = ctx.enter_context(tc.tile_pool(name="keep", bufs=1))
-        work = ctx.enter_context(tc.tile_pool(name="work", bufs=3))
+        work = ctx.enter_context(tc.tile_pool(name="work", bufs=4))
         psum = ctx.enter_context(tc.psum_pool(name="psum", bufs=2))
 
-        def kept(shape, dtype, name):
-            return keep.tile(shape, dtype, name=name, align_bytes=64)
+        def kept(shape, dtype, name, tag=""):
+            return keep.tile(shape, dtype, name=name, tag=tag, align_bytes=64)
 
-        lists = [keep.tile([P, S // 16], U16, name="list_a"), keep.tile([P, S // 16], U16, name="list_b")]
-        warm = kept([P, 16], F32, "warm")
+        def sum_bank(shape):
+            return psum.tile(shape, F32, name="sum_bank", tag="sum_bank", bufs=4)
+
+        lists = [keep.tile([P, S // 16], U16, name="list_own"), keep.tile([P, S // 16], U16, name="list_next")]
+        warm_in = kept([P, 1], F32, "warm_in", "slot_table")
+        warm_bias = kept([P, 1], F32, "warm_bias", "slot_w2")
+        warm_out = kept([P, 1], F32, "warm_out", "slot_w1")
         table_scales = kept([P, T], U8, "table_scales")
-        w1_first = kept([P, 4 * 512], F32, "w1_first")
+        w1_first = kept([P, PACK * K_PASS], F32, "w1_first")
         ident = kept([P, P], F32, "ident")
 
         nc.vector.memset(table_scales[:].bitcast(I32), 0)
-        nc.vector.memset(warm[:, 0:1], 1.0)
-        vectors = kept([P, P], F32, "vectors")
-        nc.vector.memset(vectors[:], 0.0)
+        nc.vector.memset(warm_in[:], 1.0)
+        nc.vector.memset(warm_bias[:], 1.0)
         w2_scales_raw = kept([P, H // 4], I32, "w2_scales_raw")[:]
         nc.gpsimd.memset(w2_scales_raw, 0)
         make_identity(nc, ident[:])
-        nc.scalar.activation(out=warm[:, 8:9], in_=warm[:, 0:1], func=ACT.Abs_reciprocal_sqrt)
+        nc.scalar.activation(out=warm_out[:], in_=warm_in[:], func=ACT.Abs_reciprocal_sqrt, bias=warm_bias[:])
 
         def load_scale_rows(queue, plane, rows):
             for q in range(4):
                 queue.dma_start(out=plane[32 * q : 32 * q + 4, :], in_=rows[0, 4 * q : 4 * q + 4, :].bitcast(I32))
 
         def load_w1(b, dst):
-            nc.sync.dma_start(out=dst.rearrange("p (j c) -> p j c", j=4), in_=w1[:, 512 * b : 512 * (b + 1)].rearrange("(p j) c -> p j c", j=4))
-
-        table_words = kept([P, T], U16, "table_words")
-        w2_words_hbm = w2_words[0].rearrange("p c i -> p (c i)").bitcast(I32)
-        w2_first = keep.tile([P, 512], I32, name="w2_first", tag="third", align_bytes=64)
-        w2_words_raw = [w2_first[:, 0:512]]
-        w1_second = keep.tile([P, 4 * 512], F32, name="w1_second", tag="second", align_bytes=64)
-        w1_raw = [w1_first[:], w1_second[:]]
-        nc.sync.dma_start(lists[0][:], offs)
-        nc.sync.dma_start(out=table_words[:].bitcast(I32), in_=tab_words[0].bitcast(I32))
-        nc.sync.dma_start(lists[1][:], offs2)
-        load_w1(0, w1_first[:])
-        nc.sync.dma_start(out=w2_words_raw[0], in_=w2_words_hbm[:, 0:512])
-        load_w1(1, w1_second[:])
-        load_scale_rows(nc.sync, table_scales[:].bitcast(I32), tab_scales)
-        for b in range(2):
             nc.sync.dma_start(
-                out=vectors[4 * b : 4 * b + 4, :].rearrange("t (g i) -> t g i", i=8),
-                in_=cw[512 * b : 512 * (b + 1)].rearrange("(g t i) -> t g i", t=4, i=8),
+                out=dst.rearrange("p (j c) -> p j c", j=PACK),
+                in_=w1[:, K_PASS * b : K_PASS * (b + 1)].rearrange("(p j) c -> p j c", j=PACK),
             )
-        nc.sync.dma_start(out=vectors[8:12, :], in_=gn.rearrange("(c p) -> c p", p=P))
-        load_scale_rows(nc.gpsimd, w2_scales_raw, w2_scales)
 
-        def load_w2_second():
-            raw = keep.tile([P, 512], I32, name="w2_second", tag="third", align_bytes=64)
-            nc.sync.dma_start(out=raw[:], in_=w2_words_hbm[:, 512:1024])
-            w2_words_raw.append(raw[:])
+        table_words = kept([P, T], U16, "table_words", "slot_table")
+        w2_words_hbm = w2_words[0].rearrange("p c i -> p (c i)").bitcast(I32)
+        w2_first = kept([P, K_PASS], I32, "w2_first", "slot_w2")
+        w1_second = kept([P, PACK * K_PASS], F32, "w1_second", "slot_w1")
+        w1_raw = [w1_first[:], w1_second[:]]
+        nc.sync.dma_start(lists[OWN][:], offs)
+        nc.sync.dma_start(lists[NEXT][:], offs2)
+        load_w1(0, w1_first[:])
+        load_scale_rows(nc.sync, table_scales[:].bitcast(I32), tab_scales)
+        load_w1(1, w1_second[:])
+        nc.sync.dma_start(out=table_words[:].bitcast(I32), in_=tab_words[0].bitcast(I32))
+        nc.sync.dma_start(out=w2_first[:], in_=w2_words_hbm[:, 0:K_PASS])
+        load_scale_rows(nc.gpsimd, w2_scales_raw, w2_scales)
 
         picked_words = [[], []]
         picked_scales = [[], []]
 
-        def gather(kind, a, h):
-            table, picked, dtype = ((table_scales, picked_scales, U8), (table_words, picked_words, U16))[kind]
-            name = "picked%d%d%d" % (kind, a, h)
-            dst = keep.tile([P, HALF], dtype, name=name, tag=("early%d" % a if h and kind == 0 else name), align_bytes=64)
-            nc.vector.tensor_copy(dst[:], table[:].indirect(lists[a][:, 32 * h : 32 * (h + 1)]))
+        def gather(name, table, picked, dtype, a, half):
+            dst = kept([P, HALF], dtype, "%s_%d_%d" % (name, a, half))
+            columns = slice(HALF // 16 * half, HALF // 16 * (half + 1))
+            nc.vector.tensor_copy(dst[:], table[:].indirect(lists[a][:, columns]))
             picked[a].append(dst)
 
-        w1k_bf16 = [kept([P, 2048], BF16, "w1k_bf16_%d" % b) for b in range(2)]
-        w1k_codes = [kept([P, 512], U32, "w1k_codes%d" % b) for b in range(2)]
-        w1k_plane = [kept([P, 512], U8, "w1k_plane%d" % b) for b in range(2)]
-        w1r_bf16 = [kept([P, 2048], BF16, "w1r_bf16_%d" % b) for b in range(2)]
-        w1r_codes = [kept([P, 512], U32, "w1r_codes%d" % b) for b in range(2)]
-        w1r_plane = [kept([P, 512], U8, "w1r_plane%d" % b) for b in range(2)]
+        w1k_bf16 = [kept([P, PACK * K_PASS], BF16, "w1k_bf16_%d" % b) for b in range(2)]
+        after_scales = kept([P, 4 * K_PASS + H + 4 * K], U8, "after_scales", "table_scales")
+        after_words = kept([P, K_PASS + K], U32, "after_words", "slot_table")
+        w1k_codes = [after_scales[:, 0 : 4 * K_PASS].bitcast(U32), after_words[:, 0:K_PASS]]
+        w1k_plane = [kept([P, K_PASS], U8, "w1k_plane%d" % b) for b in range(2)]
+        w1r_bf16 = [kept([P, PACK * K], BF16, "w1r_bf16_%d" % b) for b in range(2)]
+        w1r_codes = [after_scales[:, 4 * K_PASS + H :].bitcast(U32), after_words[:, K_PASS:]]
+        w1r_plane = [kept([P, K], U8, "w1r_plane%d" % b) for b in range(2)]
         w2_codes = kept([P, H], U32, "w2_codes")
-        w2_plane = keep.tile([P, H], U8, name="w2_plane", tag="w1_first", align_bytes=64)
+        w2_plane = after_scales[:, 4 * K_PASS : 4 * K_PASS + H]
 
         def round_w1(b):
-            for t in range(4):
+            for t in range(PACK):
                 nc.scalar.copy(
-                    out=w1k_bf16[b][:, 512 * t : 512 * (t + 1)].rearrange("p (g x i j) -> p g x j i", g=16, x=2, i=4, j=4),
-                    in_=w1_raw[b].rearrange("p (j g t x i) -> p t g x j i", j=4, g=16, t=4, x=2, i=4)[:, t],
+                    out=w1k_bf16[b][:, K_PASS * t : K_PASS * (t + 1)].rearrange("p (g x i j) -> p g x j i", g=16, x=2, i=4, j=PACK),
+                    in_=w1_raw[b].rearrange("p (j g t x i) -> p t g x j i", j=PACK, g=16, t=PACK, x=2, i=4)[:, t],
                 )
 
         def quantise(codes, plane, values):
             nc.vector.quantize_mx(out=codes.bitcast(FP8X4), scales=plane, in_=values)
 
         def turn_w1(b):
-            words = w1k_bf16[b][:].bitcast(F32)
+            pairs = w1k_bf16[b][:].bitcast(F32)
             for u in range(2):
-                bank = psum.tile([P, 4, P], F32, name="sum_bank", tag="sum_bank", bufs=4)
-                for t in range(4):
-                    nc.tensor.transpose(bank[:, t, :], words[:, 256 * t + u : 256 * (t + 1) : 2], ident[:])
+                bank = sum_bank([P, PACK, P])
+                for t in range(PACK):
+                    nc.tensor.transpose(bank[:, t, :], pairs[:, 2 * P * t + u : 2 * P * (t + 1) : 2], ident[:])
                 nc.scalar.copy(
-                    out=w1r_bf16[b][:].rearrange("m (p u e t) -> m u p e t", u=2, e=2, t=4)[:, u],
-                    in_=bank[:].rearrange("m t p -> m (t p)").bitcast(BF16).rearrange("m (t p e) -> m p e t", t=4, e=2),
+                    out=w1r_bf16[b][:].rearrange("m (p u e t) -> m u p e t", u=2, e=2, t=PACK)[:, u],
+                    in_=bank[:].rearrange("m t p -> m (t p)").bitcast(BF16).rearrange("m (t p e) -> m p e t", t=PACK, e=2),
                 )
 
-        def order_w2_words(b):
+        def order_w2_words(b, raw):
             nc.vector.tensor_copy(
-                out=w2_codes[:, 512 * b : 512 * (b + 1)].bitcast(I32).rearrange("p (t g i) -> p t g i", t=4, i=8),
-                in_=w2_words_raw[b].rearrange("p (g t i) -> p t g i", t=4, i=8),
+                out=w2_codes[:, K_PASS * b : K_PASS * (b + 1)].bitcast(I32).rearrange("p (t g i) -> p t g i", t=PACK, i=8),
+                in_=raw.rearrange("p (g t i) -> p t g i", t=PACK, i=8),
             )
-
-        def order_w2():
-            order_w2_words(0)
-            nc.vector.tensor_copy(
-                out=w2_plane[:].bitcast(I32).rearrange("p (b t g i) -> p b t g i", b=2, t=4, i=2),
-                in_=w2_scales_raw.rearrange("p (b g t i) -> p b t g i", b=2, t=4, i=2),
-            )
-
-        def turn_vectors():
-            bank = psum.tile([P, 4, P], F32, name="sum_bank", tag="sum_bank", bufs=4)
-            nc.tensor.transpose(bank[:, 0, :], vectors[:], ident[:])
-            nc.vector.reciprocal(out=inv_cw, in_=bank[:, 0, 0:8])
-            nc.vector.tensor_copy(out=gain, in_=bank[:, 0, 8:12])
 
         round_w1(0)
         turn_w1(0)
-        for h in range(2):
-            for a in range(2):
-                gather(1, a, h)
-        gather(0, 0, 0)
-        quantise(w1k_codes[0][:], w1k_plane[0][:], w1k_bf16[0][:])
-        gather(0, 1, 0)
-        order_w2()
-        load_w2_second()
-        per_row = keep.tile([P, 12], F32, name="per_row", tag="w1k_bf16_0", align_bytes=64)
-        inv_cw = per_row[:, 0:8]
-        gain = per_row[:, 8:12]
+        for half in range(2):
+            for a in (OWN, NEXT):
+                gather("picked_scales", table_scales, picked_scales, U8, a, half)
+        gather("picked_words", table_words, picked_words, U16, OWN, 0)
+        quantise(w1k_codes[0], w1k_plane[0][:], w1k_bf16[0][:])
+        gather("picked_words", table_words, picked_words, U16, NEXT, 0)
+        order_w2_words(0, w2_first[:])
+        nc.vector.tensor_copy(
+            out=w2_plane.bitcast(I32).rearrange("p (b t g i) -> p b t g i", b=2, t=PACK, i=2),
+            in_=w2_scales_raw.rearrange("p (b g t i) -> p b t g i", b=2, t=PACK, i=2),
+        )
+        gather("picked_words", table_words, picked_words, U16, OWN, 1)
+        gather("picked_words", table_words, picked_words, U16, NEXT, 1)
+        w2_second = kept([P, K_PASS], I32, "w2_second", "slot_w2")
+        nc.sync.dma_start(out=w2_second[:], in_=w2_words_hbm[:, K_PASS:H])
+        per_row = kept([P, 3 * PACK], F32, "per_row", "w1k_bf16_0")
+        inv_cw = per_row[:, 0 : 2 * PACK]
+        gain = per_row[:, 2 * PACK : 3 * PACK]
         round_w1(1)
-        turn_vectors()
         turn_w1(1)
-        wk_plane = keep.tile([P, K], U8, name="wk_plane", tag="third", align_bytes=64)
-        wk_codes = keep.tile([P, K], U32, name="wk_codes", tag="vectors", align_bytes=64)
 
-        def load_wk():
+        vectors = kept([P, P], F32, "vectors", "w1_first")
+        nc.gpsimd.memset(vectors[:], 0.0)
+        for b in range(2):
+            nc.sync.dma_start(
+                out=vectors[PACK * b : PACK * (b + 1), :].rearrange("t (g i) -> t g i", i=8),
+                in_=cw[K_PASS * b : K_PASS * (b + 1)].rearrange("(g t i) -> t g i", t=PACK, i=8),
+            )
+        nc.sync.dma_start(out=vectors[2 * PACK : 3 * PACK, :], in_=gn.rearrange("(c p) -> c p", p=P))
+        vector_bank = sum_bank([P, PACK, P])
+        nc.tensor.transpose(vector_bank[:, 0, :], vectors[:], ident[:])
+        nc.vector.reciprocal(out=inv_cw, in_=vector_bank[:, 0, 0 : 2 * PACK])
+        nc.vector.tensor_copy(out=gain, in_=vector_bank[:, 0, 2 * PACK : 3 * PACK])
+        wk_plane = kept([P, K], U8, "wk_plane", "slot_w2")
+        wk_codes = kept([P, K], U32, "wk_codes", "w1_first")
+
+        def prepare_second_pass():
+            order_w2_words(1, w2_second[:])
             nc.vector.memset(wk_plane[:].bitcast(I32), 0)
             load_scale_rows(nc.sync, wk_plane[:].bitcast(I32), wk_scales)
             nc.sync.dma_start(out=wk_codes[:].bitcast(I32), in_=wk_words[0].rearrange("p c i -> p (c i)").bitcast(I32))
+            quantise(w1k_codes[1], w1k_plane[1][:], w1k_bf16[1][:])
 
         units = []
         j0 = 0
         for c, width in enumerate(CHUNKS):
-            per_bank = BANK // width
+            tiles = BANK // width
             for b in range(2):
-                for t0 in range(0, 4, per_bank):
-                    units.append((c, j0, width, b, t0, per_bank))
+                for t0 in range(0, PACK, tiles):
+                    units.append((c, j0, width, b, t0, tiles))
             j0 = j0 + width
         state = {}
 
         def moving(a, j0, width):
-            h, lo = divmod(j0, HALF)
-            return picked_words[a][h][:, lo : lo + width].bitcast(FP4X4), picked_scales[a][h][:, lo : lo + width]
+            half, lo = divmod(j0, HALF)
+            return picked_words[a][half][:, lo : lo + width].bitcast(FP4X4), picked_scales[a][half][:, lo : lo + width]
 
-        def products(n):
-            c, j0, width, b, t0, per_bank = units[n]
-            own = psum.tile([P, per_bank, width], F32, name="own", tag="own")
-            nxt = psum.tile([P, per_bank, width], F32, name="nxt", tag="nxt")
-            for bank, codes, plane, base, a in ((own, w1k_codes[b], w1k_plane[b], 0, 0), (nxt, w2_codes, w2_plane, 512 * b, 1)):
-                rhs, rhs_scale = moving(a, j0, width)
-                for x in range(per_bank):
-                    cols = slice(base + P * (t0 + x), base + P * (t0 + x + 1))
-                    nc.tensor.matmul_mx(
-                        out=bank[:, x, :], lhsT=codes[:, cols].bitcast(FP8X4), lhsT_scale=plane[:, cols],
-                        rhs=rhs, rhs_scale=rhs_scale, start=True, stop=True,
-                    )
-            state[n, "own"] = own
-            state[n, "nxt"] = nxt
+        def ends_group(n):
+            return units[n][4] + units[n][5] == PACK
+
+        def product(n, a):
+            c, j0, width, b, t0, tiles = units[n]
+            name = ("own", "next")[a]
+            bank = psum.tile([P, tiles, width], F32, name=name, tag=name)
+            codes = (w1k_codes[b], w2_codes[:, K_PASS * b : K_PASS * (b + 1)])[a]
+            plane = (w1k_plane[b], w2_plane[:, K_PASS * b : K_PASS * (b + 1)])[a]
+            rhs, rhs_scale = moving(a, j0, width)
+            for x in range(tiles):
+                cols = slice(P * (t0 + x), P * (t0 + x + 1))
+                nc.tensor.matmul_mx(
+                    out=bank[:, x, :], lhsT=codes[:, cols].bitcast(FP8X4), lhsT_scale=plane[:, cols],
+                    rhs=rhs, rhs_scale=rhs_scale, start=True, stop=True,
+                )
+            state[n, name] = bank[:].rearrange("p x w -> p (x w)")
+
+        def copy_own(n):
+            own = work.tile([P, BANK], F32, name="own_sbuf", tag="own_sbuf")
+            if n < SCALAR_UNITS:
+                nc.scalar.copy(out=own[:], in_=state[n, "own"])
+            else:
+                nc.vector.tensor_copy(out=own[:], in_=state[n, "own"])
+            state[n, "own_sbuf"] = own
+
+        def next_product(n):
+            product(n, NEXT)
+            c, j0, width, b, t0, tiles = units[n]
             if t0 == 0:
-                for tag in ("d", "sq", "rs", "r2"):
-                    if n == 0 and tag == "sq":
-                        state[c, b, tag] = keep.tile([P, 4 * width], F32, name=tag, tag="second", align_bytes=64)
+                for tag in ("d", "d2", "root", "damping"):
+                    if n == 0 and tag == "d2":
+                        state[c, b, tag] = kept([P, PACK * width], F32, tag, "slot_w1")
                     else:
-                        state[c, b, tag] = work.tile([P, 4 * width], F32, name=tag, tag=tag, bufs=4)
+                        state[c, b, tag] = work.tile([P, PACK * width], F32, name=tag, tag=tag)
 
-        def part(n, tag):
-            c, j0, width, b, t0, per_bank = units[n]
-            return state[c, b, tag][:, t0 * width : (t0 + per_bank) * width]
-
-        def flat(bank):
-            return bank[:].rearrange("p x w -> p (x w)")
-
-        def leave(n):
-            if n in HOLD:
-                succ = keep.tile([P, BANK], F32, name="succ", tag="early%d" % HOLD.index(n), align_bytes=64)
-            else:
-                succ = work.tile([P, BANK], F32, name="succ", tag="succ", bufs=4)
-            if P1_ENG[n] == "v":
-                nc.vector.tensor_copy(out=succ[:], in_=flat(state[n, "own"]))
-            else:
-                nc.scalar.copy(out=succ[:], in_=flat(state[n, "own"]))
-            state[n, "succ"] = succ
+        def span(run, tag):
+            c, j0, width, b, t0, tiles = units[run[0]]
+            return state[c, b, tag][:, t0 * width : (t0 + len(run) * tiles) * width]
 
         def subtract(n):
-            nc.vector.tensor_tensor(out=part(n, "d"), in0=state[n, "succ"][:], in1=flat(state[n, "nxt"]), op=ALU.subtract)
+            nc.vector.tensor_tensor(out=span([n], "d"), in0=state[n, "own_sbuf"][:], in1=state[n, "next"], op=ALU.subtract)
 
-        def square(eng, dst, src):
-            if eng == "s":
-                nc.scalar.activation(out=dst, in_=src, func=ACT.Square)
-            elif eng == "v":
-                nc.vector.tensor_tensor(out=dst, in0=src, in1=src, op=ALU.mult)
-            else:
-                nc.gpsimd.tensor_tensor(out=dst, in0=src, in1=src, op=ALU.mult)
+        def scalar_run(n):
+            if n < 2 or n >= len(units) - 2:
+                return [n]
+            return [n - 1, n] if n % 2 == 1 else []
 
-        def damp(n):
-            c, j0, width, b, t0, per_bank = units[n]
-            for t in range(t0, t0 + per_bank):
-                cols = slice(t * width, (t + 1) * width)
-                nc.scalar.activation(
-                    out=state[c, b, "rs"][:, cols], in_=state[c, b, "sq"][:, cols], func=ACT.Abs_reciprocal_sqrt,
-                    bias=inv_cw[:, 4 * b + t : 4 * b + t + 1],
-                )
+        def square(n, dst, src):
+            run = scalar_run(n)
+            if run:
+                nc.scalar.activation(out=span(run, dst), in_=span(run, src), func=ACT.Square)
+
+        def inverse_root(n):
+            for m in scalar_run(n):
+                c, j0, width, b, t0, tiles = units[m]
+                for t in range(t0, t0 + tiles):
+                    cols = slice(t * width, (t + 1) * width)
+                    nc.scalar.activation(
+                        out=state[c, b, "root"][:, cols], in_=state[c, b, "d2"][:, cols], func=ACT.Abs_reciprocal_sqrt,
+                        bias=inv_cw[:, PACK * b + t : PACK * b + t + 1],
+                    )
 
         def weave(n):
-            c, j0, width, b, t0, per_bank = units[n]
-            if t0 + per_bank < 4:
+            if not ends_group(n):
                 return
-            h_bf16 = work.tile([P, 4 * width], BF16, name="h_bf16", tag="h_bf16", bufs=2, align_bytes=64)
-            eng = nc.vector if P6_ENG[2 * c + b] == "v" else nc.gpsimd
-            run = RUN if P6_ENG[2 * c + b] == "g" else 2
-            step = PIECE if P6_ENG[2 * c + b] == "g" else 256
-            for lo in range(0, width, step):
-                hi = min(width, lo + step)
-                eng.tensor_tensor(
-                    out=h_bf16[:, 4 * lo : 4 * hi].rearrange("p (c i t) -> p c t i", i=run, t=4),
-                    in0=state[c, b, "d"][:].rearrange("p (t c i) -> p c t i", t=4, i=run)[:, lo // run : hi // run],
-                    in1=state[c, b, "r2"][:].rearrange("p (t c i) -> p c t i", t=4, i=run)[:, lo // run : hi // run],
+            c, j0, width, b, t0, tiles = units[n]
+            h_bf16 = work.tile([P, PACK * width], BF16, name="h_bf16", tag="h_bf16", bufs=2, align_bytes=64)
+            for lo in range(0, width, WEAVE):
+                pairs = slice(lo // 2, (lo + WEAVE) // 2)
+                nc.vector.tensor_tensor(
+                    out=h_bf16[:, PACK * lo : PACK * (lo + WEAVE)].rearrange("p (c i t) -> p c t i", i=2, t=PACK),
+                    in0=state[c, b, "d"][:].rearrange("p (t c i) -> p c t i", t=PACK, i=2)[:, pairs],
+                    in1=state[c, b, "damping"][:].rearrange("p (t c i) -> p c t i", t=PACK, i=2)[:, pairs],
                     op=ALU.mult,
                 )
             state[c, b, "h"] = h_bf16
 
-        def back(n):
-            c, j0, width, b, t0, per_bank = units[n]
-            if t0 + per_bank < 4:
+        def quantise_h(n):
+            if not ends_group(n):
                 return
+            c, j0, width, b, t0, tiles = units[n]
             h_codes = work.tile([P, width], U32, name="h_codes", tag="h_codes", bufs=3, align_bytes=64)
             h_plane = work.tile([P, width], U8, name="h_plane", tag="h_plane", bufs=3, align_bytes=64)
             if c == 0:
-                quantise(w1r_codes[b][:], w1r_plane[b][:], w1r_bf16[b][:])
+                quantise(w1r_codes[b], w1r_plane[b][:], w1r_bf16[b][:])
             quantise(h_codes[:], h_plane[:], state[c, b, "h"][:])
-            state[c, b, "hq"] = (h_codes, h_plane)
+            state[c, b, "h_mx"] = (h_codes, h_plane)
 
-        def passes(c, j0, width, bb, nt):
-            cols = slice(P * nt, P * (nt + 1))
-            if bb == 0:
-                state[c, nt, "y"] = psum.tile([P, width], F32, name="sum_bank", tag="sum_bank", bufs=4)
-            y = state[c, nt, "y"]
-            codes, plane = state[c, bb, "hq"]
-            nc.tensor.matmul_mx(
-                out=y[:], lhsT=w1r_codes[bb][:, cols].bitcast(FP8X4), lhsT_scale=w1r_plane[bb][:, cols],
-                rhs=codes[:].bitcast(FP8X4), rhs_scale=plane[:], start=(bb == 0), stop=(bb == 1),
-            )
-            if bb == 0:
-                step = BANK if width == BANK else P
-                for lo in range(0, width, step):
-                    rhs, rhs_scale = moving(0, j0 + lo, step)
-                    nc.tensor.matmul_mx(
-                        out=y[:, lo : lo + step], lhsT=wk_codes[:, cols].bitcast(FP8X4), lhsT_scale=wk_plane[:, cols],
-                        rhs=rhs, rhs_scale=rhs_scale, start=False, stop=False,
-                    )
-
-        def finish(c, j0, width, nt):
-            result = work.tile([P, width], F32, name="result", tag="result", bufs=4)
-            if OUT_ENG[4 * c + nt] == "v":
-                nc.vector.tensor_scalar(
-                    out=result[:], in0=state[c, nt, "y"][:], scalar1=gain[:, nt : nt + 1], scalar2=None, op0=ALU.mult
+        def second_product(n, row_tiles):
+            if not ends_group(n):
+                return
+            c, j0, width, b, t0, tiles = units[n]
+            h_codes, h_plane = state[c, b, "h_mx"]
+            for nt in row_tiles:
+                cols = slice(P * nt, P * (nt + 1))
+                if b == 0:
+                    state[c, nt, "y"] = sum_bank([P, width])
+                y = state[c, nt, "y"]
+                nc.tensor.matmul_mx(
+                    out=y[:], lhsT=w1r_codes[b][:, cols].bitcast(FP8X4), lhsT_scale=w1r_plane[b][:, cols],
+                    rhs=h_codes[:].bitcast(FP8X4), rhs_scale=h_plane[:], start=(b == 0), stop=(b == 1),
                 )
-            else:
-                nc.scalar.activation(out=result[:], in_=state[c, nt, "y"][:], func=ACT.Copy, scale=gain[:, nt : nt + 1])
-            nc.sync.dma_start(out=out[P * nt : P * (nt + 1), j0 : j0 + width], in_=result[:])
+                if b == 0:
+                    skip_width = BANK if width == BANK else P
+                    for lo in range(0, width, skip_width):
+                        rhs, rhs_scale = moving(OWN, j0 + lo, skip_width)
+                        nc.tensor.matmul_mx(
+                            out=y[:, lo : lo + skip_width], lhsT=wk_codes[:, cols].bitcast(FP8X4), lhsT_scale=wk_plane[:, cols],
+                            rhs=rhs, rhs_scale=rhs_scale, start=False, stop=False,
+                        )
 
-        def span(n, tag, count):
-            c, j0, width, b, t0, per_bank = units[n]
-            return state[c, b, tag][:, (t0 + per_bank - count * per_bank) * width : (t0 + per_bank) * width]
-
-        def wide_square(n, engines, dst, src):
-            if WIDE[n] == "1":
-                square(engines[n], span(n, dst, 1), span(n, src, 1))
-            elif n % 2 == 1:
-                square(engines[n], span(n, dst, 2), span(n, src, 2))
-
-        def wide_damp(n):
-            if WIDE[n] == "1":
-                damp(n)
-            elif n % 2 == 1:
-                damp(n - 1)
-                damp(n)
-
-        def second_product(n, part_no):
-            c, j0, width, b, t0, per_bank = units[n]
-            if t0 + per_bank < 4:
+        def store(n, row_tiles):
+            c, j0, width, b, t0, tiles = units[n]
+            if not ends_group(n) or b == 0:
                 return
-            for nt in range(2 * part_no, 2 * part_no + 2):
-                passes(c, j0, width, b, nt)
-
-        def results(n, part_no):
-            c, j0, width, b, t0, per_bank = units[n]
-            if t0 + per_bank < 4 or b == 0:
-                return
-            for nt in range(2 * part_no, 2 * part_no + 2):
-                finish(c, j0, width, nt)
+            for nt in row_tiles:
+                result = work.tile([P, width], F32, name="result", tag="result")
+                y = state[c, nt, "y"]
+                if c == 0 or nt % 2 == 0:
+                    nc.vector.tensor_scalar(out=result[:], in0=y[:], scalar1=gain[:, nt : nt + 1], scalar2=None, op0=ALU.mult)
+                else:
+                    nc.scalar.activation(out=result[:], in_=y[:], func=ACT.Copy, scale=gain[:, nt : nt + 1])
+                nc.sync.dma_start(out=out[P * nt : P * (nt + 1), j0 : j0 + width], in_=result[:])
 
         stages = [
-            products,
-            leave,
+            lambda n: product(n, OWN),
+            copy_own,
+            next_product,
             subtract,
-            lambda n: wide_square(n, P3_ENG, "sq", "d"),
-            wide_damp,
-            lambda n: wide_square(n, P5_ENG, "r2", "rs"),
+            lambda n: square(n, "d2", "d"),
+            inverse_root,
+            lambda n: square(n, "damping", "root"),
             weave,
-            back,
-            lambda n: second_product(n, 0),
-            lambda n: second_product(n, 1),
-            lambda n: results(n, 0),
-            lambda n: results(n, 1),
+            quantise_h,
+            lambda n: second_product(n, (0, 1)),
+            lambda n: second_product(n, (2, 3)),
+            lambda n: store(n, (0, 1)),
+            lambda n: store(n, (2, 3)),
         ]
-        for step in range(len(units) + max(LAGS)):
-            if step == 2:
-                order_w2_words(1)
-                load_wk()
-                quantise(w1k_codes[1][:], w1k_plane[1][:], w1k_bf16[1][:])
-            for lag, stage in zip(LAGS, stages):
+        lags = [0, 1] + [1 + LEAD + x for x in range(len(stages) - 2)]
+        first_of_second_pass = PACK // units[0][5]
+        for step in range(len(units) + lags[-1]):
+            if step == first_of_second_pass // 2:
+                prepare_second_pass()
+            for lag, stage in zip(lags, stages):
                 if 0 <= step - lag < len(units):
                     stage(step - lag)
-            if step - LAGS[2] in HOLD:
-                gather(HOLD.index(step - LAGS[2]) // 2, HOLD.index(step - LAGS[2]) % 2, 1)

from contextlib import ExitStack

import concourse.mybir as mybir
from concourse.masks import make_identity

K, H, T, S = 512, 1024, 4096, 1024
FLOPS = 2 * S * (2 * K * H + H * K + K * K)

F32 = mybir.dt.float32
BF16 = mybir.dt.bfloat16
I32 = mybir.dt.int32
U32 = mybir.dt.uint32
U16 = mybir.dt.uint16
U8 = mybir.dt.uint8
FP8X4 = mybir.dt.float8_e4m3fn_x4
FP4X4 = mybir.dt.float4_e2m1fn_x4
ALU = mybir.AluOpType
ACT = mybir.ActivationFunctionType

P = 128
PACK = 4
K_PASS = P * PACK
BANK = 512
HALF = S // 2
CHUNKS = [512, 256, 256]
SCALAR_UNITS = 5
LEAD = 3
WEAVE = 256
OWN, NEXT = 0, 1


def tile_list_segment_successor_refinement_kernel(
    tc, tab_words, tab_scales, offs, offs2, w1, w2_words, w2_scales, wk_words, wk_scales, cw, gn, out
):
    nc = tc.nc
    with ExitStack() as ctx:
        keep = ctx.enter_context(tc.tile_pool(name="keep", bufs=1))
        work = ctx.enter_context(tc.tile_pool(name="work", bufs=4))
        psum = ctx.enter_context(tc.psum_pool(name="psum", bufs=2))

        def kept(shape, dtype, name, tag=""):
            return keep.tile(shape, dtype, name=name, tag=tag, align_bytes=64)

        def sum_bank(shape):
            return psum.tile(shape, F32, name="sum_bank", tag="sum_bank", bufs=4)

        lists = [keep.tile([P, S // 16], U16, name="list_own"), keep.tile([P, S // 16], U16, name="list_next")]
        warm_in = kept([P, 1], F32, "warm_in", "slot_table")
        warm_bias = kept([P, 1], F32, "warm_bias", "slot_w2")
        warm_out = kept([P, 1], F32, "warm_out", "slot_w1")
        table_scales = kept([P, T], U8, "table_scales")
        w1_first = kept([P, PACK * K_PASS], F32, "w1_first")
        ident = kept([P, P], F32, "ident")

        nc.vector.memset(table_scales[:].bitcast(I32), 0)
        nc.vector.memset(warm_in[:], 1.0)
        nc.vector.memset(warm_bias[:], 1.0)
        w2_scales_raw = kept([P, H // 4], I32, "w2_scales_raw")[:]
        nc.gpsimd.memset(w2_scales_raw, 0)
        make_identity(nc, ident[:])
        nc.scalar.activation(out=warm_out[:], in_=warm_in[:], func=ACT.Abs_reciprocal_sqrt, bias=warm_bias[:])

        def load_scale_rows(queue, plane, rows):
            for q in range(4):
                queue.dma_start(out=plane[32 * q : 32 * q + 4, :], in_=rows[0, 4 * q : 4 * q + 4, :].bitcast(I32))

        def load_w1(b, dst):
            nc.sync.dma_start(
                out=dst.rearrange("p (j c) -> p j c", j=PACK),
                in_=w1[:, K_PASS * b : K_PASS * (b + 1)].rearrange("(p j) c -> p j c", j=PACK),
            )

        table_words = kept([P, T], U16, "table_words", "slot_table")
        w2_words_hbm = w2_words[0].rearrange("p c i -> p (c i)").bitcast(I32)
        w2_first = kept([P, K_PASS], I32, "w2_first", "slot_w2")
        w1_second = kept([P, PACK * K_PASS], F32, "w1_second", "slot_w1")
        w1_raw = [w1_first[:], w1_second[:]]
        nc.sync.dma_start(lists[OWN][:], offs)
        nc.sync.dma_start(lists[NEXT][:], offs2)
        load_w1(0, w1_first[:])
        load_scale_rows(nc.sync, table_scales[:].bitcast(I32), tab_scales)
        load_w1(1, w1_second[:])
        nc.sync.dma_start(out=table_words[:].bitcast(I32), in_=tab_words[0].bitcast(I32))
        nc.sync.dma_start(out=w2_first[:], in_=w2_words_hbm[:, 0:K_PASS])
        load_scale_rows(nc.gpsimd, w2_scales_raw, w2_scales)

        picked_words = [[], []]
        picked_scales = [[], []]

        def gather(name, table, picked, dtype, a, half):
            dst = kept([P, HALF], dtype, "%s_%d_%d" % (name, a, half))
            columns = slice(HALF // 16 * half, HALF // 16 * (half + 1))
            nc.vector.tensor_copy(dst[:], table[:].indirect(lists[a][:, columns]))
            picked[a].append(dst)

        w1k_bf16 = [kept([P, PACK * K_PASS], BF16, "w1k_bf16_%d" % b) for b in range(2)]
        after_scales = kept([P, 4 * K_PASS + H + 4 * K], U8, "after_scales", "table_scales")
        after_words = kept([P, K_PASS + K], U32, "after_words", "slot_table")
        w1k_codes = [after_scales[:, 0 : 4 * K_PASS].bitcast(U32), after_words[:, 0:K_PASS]]
        w1k_plane = [kept([P, K_PASS], U8, "w1k_plane%d" % b) for b in range(2)]
        w1r_bf16 = [kept([P, PACK * K], BF16, "w1r_bf16_%d" % b) for b in range(2)]
        w1r_codes = [after_scales[:, 4 * K_PASS + H :].bitcast(U32), after_words[:, K_PASS:]]
        w1r_plane = [kept([P, K], U8, "w1r_plane%d" % b) for b in range(2)]
        w2_codes = kept([P, H], U32, "w2_codes")
        w2_plane = after_scales[:, 4 * K_PASS : 4 * K_PASS + H]

        def round_w1(b):
            for t in range(PACK):
                nc.scalar.copy(
                    out=w1k_bf16[b][:, K_PASS * t : K_PASS * (t + 1)].rearrange("p (g x i j) -> p g x j i", g=16, x=2, i=4, j=PACK),
                    in_=w1_raw[b].rearrange("p (j g t x i) -> p t g x j i", j=PACK, g=16, t=PACK, x=2, i=4)[:, t],
                )

        def quantise(codes, plane, values):
            nc.vector.quantize_mx(out=codes.bitcast(FP8X4), scales=plane, in_=values)

        def turn_w1(b):
            pairs = w1k_bf16[b][:].bitcast(F32)
            for u in range(2):
                bank = sum_bank([P, PACK, P])
                for t in range(PACK):
                    nc.tensor.transpose(bank[:, t, :], pairs[:, 2 * P * t + u : 2 * P * (t + 1) : 2], ident[:])
                nc.scalar.copy(
                    out=w1r_bf16[b][:].rearrange("m (p u e t) -> m u p e t", u=2, e=2, t=PACK)[:, u],
                    in_=bank[:].rearrange("m t p -> m (t p)").bitcast(BF16).rearrange("m (t p e) -> m p e t", t=PACK, e=2),
                )

        def order_w2_words(b, raw):
            nc.vector.tensor_copy(
                out=w2_codes[:, K_PASS * b : K_PASS * (b + 1)].bitcast(I32).rearrange("p (t g i) -> p t g i", t=PACK, i=8),
                in_=raw.rearrange("p (g t i) -> p t g i", t=PACK, i=8),
            )

        round_w1(0)
        turn_w1(0)
        for half in range(2):
            for a in (OWN, NEXT):
                gather("picked_scales", table_scales, picked_scales, U8, a, half)
        gather("picked_words", table_words, picked_words, U16, OWN, 0)
        quantise(w1k_codes[0], w1k_plane[0][:], w1k_bf16[0][:])
        gather("picked_words", table_words, picked_words, U16, NEXT, 0)
        order_w2_words(0, w2_first[:])
        nc.vector.tensor_copy(
            out=w2_plane.bitcast(I32).rearrange("p (b t g i) -> p b t g i", b=2, t=PACK, i=2),
            in_=w2_scales_raw.rearrange("p (b g t i) -> p b t g i", b=2, t=PACK, i=2),
        )
        gather("picked_words", table_words, picked_words, U16, OWN, 1)
        gather("picked_words", table_words, picked_words, U16, NEXT, 1)
        w2_second = kept([P, K_PASS], I32, "w2_second", "slot_w2")
        nc.sync.dma_start(out=w2_second[:], in_=w2_words_hbm[:, K_PASS:H])
        per_row = kept([P, 3 * PACK], F32, "per_row", "w1k_bf16_0")
        inv_cw = per_row[:, 0 : 2 * PACK]
        gain = per_row[:, 2 * PACK : 3 * PACK]
        round_w1(1)
        turn_w1(1)

        vectors = kept([P, P], F32, "vectors", "w1_first")
        nc.gpsimd.memset(vectors[:], 0.0)
        for b in range(2):
            nc.sync.dma_start(
                out=vectors[PACK * b : PACK * (b + 1), :].rearrange("t (g i) -> t g i", i=8),
                in_=cw[K_PASS * b : K_PASS * (b + 1)].rearrange("(g t i) -> t g i", t=PACK, i=8),
            )
        nc.sync.dma_start(out=vectors[2 * PACK : 3 * PACK, :], in_=gn.rearrange("(c p) -> c p", p=P))
        vector_bank = sum_bank([P, PACK, P])
        nc.tensor.transpose(vector_bank[:, 0, :], vectors[:], ident[:])
        nc.vector.reciprocal(out=inv_cw, in_=vector_bank[:, 0, 0 : 2 * PACK])
        nc.vector.tensor_copy(out=gain, in_=vector_bank[:, 0, 2 * PACK : 3 * PACK])
        wk_plane = kept([P, K], U8, "wk_plane", "slot_w2")
        wk_codes = kept([P, K], U32, "wk_codes", "w1_first")

        def prepare_second_pass():
            order_w2_words(1, w2_second[:])
            nc.vector.memset(wk_plane[:].bitcast(I32), 0)
            load_scale_rows(nc.sync, wk_plane[:].bitcast(I32), wk_scales)
            nc.sync.dma_start(out=wk_codes[:].bitcast(I32), in_=wk_words[0].rearrange("p c i -> p (c i)").bitcast(I32))
            quantise(w1k_codes[1], w1k_plane[1][:], w1k_bf16[1][:])

        units = []
        j0 = 0
        for c, width in enumerate(CHUNKS):
            tiles = BANK // width
            for b in range(2):
                for t0 in range(0, PACK, tiles):
                    units.append((c, j0, width, b, t0, tiles))
            j0 = j0 + width
        state = {}

        def moving(a, j0, width):
            half, lo = divmod(j0, HALF)
            return picked_words[a][half][:, lo : lo + width].bitcast(FP4X4), picked_scales[a][half][:, lo : lo + width]

        def ends_group(n):
            return units[n][4] + units[n][5] == PACK

        def product(n, a):
            c, j0, width, b, t0, tiles = units[n]
            name = ("own", "next")[a]
            bank = psum.tile([P, tiles, width], F32, name=name, tag=name)
            codes = (w1k_codes[b], w2_codes[:, K_PASS * b : K_PASS * (b + 1)])[a]
            plane = (w1k_plane[b], w2_plane[:, K_PASS * b : K_PASS * (b + 1)])[a]
            rhs, rhs_scale = moving(a, j0, width)
            for x in range(tiles):
                cols = slice(P * (t0 + x), P * (t0 + x + 1))
                nc.tensor.matmul_mx(
                    out=bank[:, x, :], lhsT=codes[:, cols].bitcast(FP8X4), lhsT_scale=plane[:, cols],
                    rhs=rhs, rhs_scale=rhs_scale, start=True, stop=True,
                )
            state[n, name] = bank[:].rearrange("p x w -> p (x w)")

        def copy_own(n):
            own = work.tile([P, BANK], F32, name="own_sbuf", tag="own_sbuf")
            if n < SCALAR_UNITS:
                nc.scalar.copy(out=own[:], in_=state[n, "own"])
            else:
                nc.vector.tensor_copy(out=own[:], in_=state[n, "own"])
            state[n, "own_sbuf"] = own

        def next_product(n):
            product(n, NEXT)
            c, j0, width, b, t0, tiles = units[n]
            if t0 == 0:
                for tag in ("d", "d2", "root", "damping"):
                    if n == 0 and tag == "d2":
                        state[c, b, tag] = kept([P, PACK * width], F32, tag, "slot_w1")
                    else:
                        state[c, b, tag] = work.tile([P, PACK * width], F32, name=tag, tag=tag)

        def span(run, tag):
            c, j0, width, b, t0, tiles = units[run[0]]
            return state[c, b, tag][:, t0 * width : (t0 + len(run) * tiles) * width]

        def subtract(n):
            nc.vector.tensor_tensor(out=span([n], "d"), in0=state[n, "own_sbuf"][:], in1=state[n, "next"], op=ALU.subtract)

        def scalar_run(n):
            if n < 2 or n >= len(units) - 2:
                return [n]
            return [n - 1, n] if n % 2 == 1 else []

        def square(n, dst, src):
            run = scalar_run(n)
            if run:
                nc.scalar.activation(out=span(run, dst), in_=span(run, src), func=ACT.Square)

        def inverse_root(n):
            for m in scalar_run(n):
                c, j0, width, b, t0, tiles = units[m]
                for t in range(t0, t0 + tiles):
                    cols = slice(t * width, (t + 1) * width)
                    nc.scalar.activation(
                        out=state[c, b, "root"][:, cols], in_=state[c, b, "d2"][:, cols], func=ACT.Abs_reciprocal_sqrt,
                        bias=inv_cw[:, PACK * b + t : PACK * b + t + 1],
                    )

        def weave(n):
            if not ends_group(n):
                return
            c, j0, width, b, t0, tiles = units[n]
            h_bf16 = work.tile([P, PACK * width], BF16, name="h_bf16", tag="h_bf16", bufs=2, align_bytes=64)
            for lo in range(0, width, WEAVE):
                pairs = slice(lo // 2, (lo + WEAVE) // 2)
                nc.vector.tensor_tensor(
                    out=h_bf16[:, PACK * lo : PACK * (lo + WEAVE)].rearrange("p (c i t) -> p c t i", i=2, t=PACK),
                    in0=state[c, b, "d"][:].rearrange("p (t c i) -> p c t i", t=PACK, i=2)[:, pairs],
                    in1=state[c, b, "damping"][:].rearrange("p (t c i) -> p c t i", t=PACK, i=2)[:, pairs],
                    op=ALU.mult,
                )
            state[c, b, "h"] = h_bf16

        def quantise_h(n):
            if not ends_group(n):
                return
            c, j0, width, b, t0, tiles = units[n]
            h_codes = work.tile([P, width], U32, name="h_codes", tag="h_codes", bufs=3, align_bytes=64)
            h_plane = work.tile([P, width], U8, name="h_plane", tag="h_plane", bufs=3, align_bytes=64)
            if c == 0:
                quantise(w1r_codes[b], w1r_plane[b][:], w1r_bf16[b][:])
            quantise(h_codes[:], h_plane[:], state[c, b, "h"][:])
            state[c, b, "h_mx"] = (h_codes, h_plane)

        def second_product(n, row_tiles):
            if not ends_group(n):
                return
            c, j0, width, b, t0, tiles = units[n]
            h_codes, h_plane = state[c, b, "h_mx"]
            for nt in row_tiles:
                cols = slice(P * nt, P * (nt + 1))
                if b == 0:
                    state[c, nt, "y"] = sum_bank([P, width])
                y = state[c, nt, "y"]
                nc.tensor.matmul_mx(
                    out=y[:], lhsT=w1r_codes[b][:, cols].bitcast(FP8X4), lhsT_scale=w1r_plane[b][:, cols],
                    rhs=h_codes[:].bitcast(FP8X4), rhs_scale=h_plane[:], start=(b == 0), stop=(b == 1),
                )
                if b == 0:
                    skip_width = BANK if width == BANK else P
                    for lo in range(0, width, skip_width):
                        rhs, rhs_scale = moving(OWN, j0 + lo, skip_width)
                        nc.tensor.matmul_mx(
                            out=y[:, lo : lo + skip_width], lhsT=wk_codes[:, cols].bitcast(FP8X4), lhsT_scale=wk_plane[:, cols],
                            rhs=rhs, rhs_scale=rhs_scale, start=False, stop=False,
                        )

        def store(n, row_tiles):
            c, j0, width, b, t0, tiles = units[n]
            if not ends_group(n) or b == 0:
                return
            for nt in row_tiles:
                result = work.tile([P, width], F32, name="result", tag="result")
                y = state[c, nt, "y"]
                if c == 0 or nt % 2 == 0:
                    nc.vector.tensor_scalar(out=result[:], in0=y[:], scalar1=gain[:, nt : nt + 1], scalar2=None, op0=ALU.mult)
                else:
                    nc.scalar.activation(out=result[:], in_=y[:], func=ACT.Copy, scale=gain[:, nt : nt + 1])
                nc.sync.dma_start(out=out[P * nt : P * (nt + 1), j0 : j0 + width], in_=result[:])

        stages = [
            lambda n: product(n, OWN),
            copy_own,
            next_product,
            subtract,
            lambda n: square(n, "d2", "d"),
            inverse_root,
            lambda n: square(n, "damping", "root"),
            weave,
            quantise_h,
            lambda n: second_product(n, (0, 1)),
            lambda n: second_product(n, (2, 3)),
            lambda n: store(n, (0, 1)),
            lambda n: store(n, (2, 3)),
        ]
        lags = [0, 1] + [1 + LEAD + x for x in range(len(stages) - 2)]
        first_of_second_pass = PACK // units[0][5]
        for step in range(len(units) + lags[-1]):
            if step == first_of_second_pass // 2:
                prepare_second_pass()
            for lag, stage in zip(lags, stages):
                if 0 <= step - lag < len(units):
                    stage(step - lag)
